import numpy as np, ml_dtypes
CORES = [24,25,26,27,48,49,50,51,72,73,74,75,96,97,98,99]
N = 16
RM, R, T = 262144, 16384, 2048
CAPP = 256
def entries(a): return a.T.reshape(-1)
def pack(v, P): return np.ascontiguousarray(np.asarray(v, np.int32).reshape(-1, P).T)
def owners(rng, how):
    if how == "alike": return np.stack([rng.permutation(np.repeat(rng.permutation(N)[:T // CAPP], CAPP)) for r in range(N)])
    if how == "full": p = np.repeat(rng.permutation(N)[:T // CAPP], CAPP); return np.stack([rng.permutation(p) for r in range(N)])
    return np.stack([rng.permutation(np.repeat(np.arange(N), CAPP))[:T] for r in range(N)])
def lists(rng, how):
    M = rng.integers(0, N * R, N * RM)
    O1 = owners(rng, how); O2 = rng.permutation(N)[O1] if how in ("alike", "full") else owners(rng, "uniform")
    sl = np.stack([1 + rng.permutation(RM - 2)[:N * T] for o in range(N)])
    if how == "edge": sl[:, 0] = 0; sl[:, 1] = RM - 1
    I = np.zeros((N, T), np.int64); took = np.zeros(N, np.int64)
    for r in range(N):
        for o in range(N): m = np.nonzero(O1[r] == o)[0]; I[r, m] = RM * o + sl[o, took[o]:took[o] + len(m)]; took[o] += len(m)
    A = R * O2 + (np.where(rng.random((N, T)) < 0.5, 0, R - 1) if how == "edge" else rng.integers(0, R, (N, T)))
    if how == "alike": I = RM * O1 + sl[O1, 0]; A = R * O2 + rng.integers(0, R, N)[O1]
    M[I.reshape(-1)] = A.reshape(-1)
    if how == "sorted": I = np.sort(I, axis=1)
    if how == "full":
        I[1::3] = np.sort(I[1::3], axis=1); I[2::3] = np.sort(I[2::3], axis=1).reshape(-1, 16, T // 16).transpose(0, 2, 1).reshape(-1, T)
    return {"mp": np.stack([pack(m, 16) for m in M.reshape(N, RM)]), "idx": np.stack([pack(i, 16) for i in I])}
def setup_inputs(rng):
    return dict({"tab": rng.standard_normal((N, 128, R), dtype=np.float32).astype(ml_dtypes.bfloat16)}, **lists(rng, "uniform"))
def setup_inputs_alike(rng):
    d = setup_inputs(rng); d.update(lists(rng, "alike"))
    for k in ("tab",): d[k] = (d[k].astype(np.float32) * 1048576.0).astype(d[k].dtype)
    return d
def setup_inputs_edge(rng):
    d = setup_inputs(rng); d.update(lists(rng, "edge"))
    for k in ("tab",): d[k] = (d[k].astype(np.float32) * (1 / 1024.0)).astype(d[k].dtype)
    return d
def setup_inputs_full(rng):
    d = setup_inputs(rng); d.update(lists(rng, "full"))
    return d
def setup_inputs_sorted(rng):
    d = setup_inputs(rng); d.update(lists(rng, "sorted"))
    return d
def check_inputs(x):
    bad = []
    if x["mp"].min() < 0 or x["mp"].max() >= N * R: bad.append("mp out of range")
    if x["idx"].min() < 0 or x["idx"].max() >= N * RM: bad.append("idx out of range")
    M = np.concatenate([entries(m) for m in x["mp"]])
    if max(int(np.bincount(entries(a) // RM, minlength=N).max()) for a in x["idx"]) > CAPP: bad.append("more than CAPP entries of a list point into one rank's part of the map")
    if max(int(np.bincount(M[entries(a)] // R, minlength=N).max()) for a in x["idx"]) > CAPP: bad.append("more than CAPP entries of a list have map values in one rank's part of the table")
    return bad
def reference(tab, mp, idx):
    A = np.concatenate(list(tab), axis=1)
    M = np.concatenate([entries(m) for m in mp])
    return {"y": np.stack([A[:, M[entries(idx[r])]] for r in range(N)])}

@@ -1,0 +1,400 @@
+from concourse.bass import DstId, RemoteDMATransfer
+from concourse.mybir import AluOpType as OP, AxisListType, ActivationFunctionType as AF
+
+NC = 112
+MSH, TSH = 18, 14
+BIAS = float((1 << 17) + 256)
+PE_SC = 5
+
+SCRATCH = {
+    "x": ("sbuf", [128, 16], "int32"), "win": ("sbuf", [128, 8192], "int32"), "tabs": ("sbuf", [128, 16384], "bfloat16"),
+    "recv": ("sbuf", [128, 4096], "bfloat16"), "gout": ("sbuf", [128, 4096], "bfloat16"), "ys": ("sbuf", [128, 2048], "bfloat16"),
+    "rel": ("sbuf", [128, 1024], "bfloat16"), "slu": ("sbuf", [128, 16], "uint16"), "yoff": ("sbuf", [128, 128], "uint16"),
+    "ysl": ("dram", [16, 128], "uint16"), "pst": ("psum", [128, 2048], "bfloat16"),
+    "q1": ("sbuf", [128, 32], "int32"), "q2": ("sbuf", [128, 32], "int32"), "q3": ("sbuf", [128, 32], "float32"),
+    "gw1": ("sbuf", [128, 32], "int32"), "gw2": ("sbuf", [128, 32], "int32"), "gw3": ("sbuf", [128, 32], "float32"),
+    "l1": ("sbuf", [128, 128], "int32"), "l2": ("sbuf", [128, 128], "int32"), "l3": ("sbuf", [128, 128], "float32"),
+}
+for _n in ("psb", "pse", "psu0", "psu1", "psd", "psf"):
+    SCRATCH[_n] = ("psum", [128, 512], "float32")
+_INT = dict(ip=16, ip15=16, b32=32, ci=32, yq=32, yh=32, ya=32, yb=32, mh=32, ml=32, m=16)
+_FLT = dict(pcol=16, p16=16, key=256, su=256, key8=1024, s8=1024, lpat=512, dmask=512, g16=16, hi01=16, cf=32, gat=1024, gt=1024,
+            ff=512, f1=256, f2=128, f3=64, pr=512, junk=512, mf=16, o256=16, sl=16)
+_BF = dict(iom=128, opat=256, tpat=256, d0=256, low=128, ident=128, at=2048, b01=512, hb=32, lb=32)
+_U16 = dict(offt=16, coff=64, o2=32, off=256)
+for _f in "12":
+    for _n in ("own", "ow2", "hh", "ll"):
+        _INT[_n + _f] = 16
+    for _n in ("cb4", "cb", "vh", "vl", "rk", "ge4", "gm", "hi", "lo", "nlo"):
+        _FLT[_n + _f] = 16
+    for _n, _w in dict(oh=256, s1=256, ohb=256, cc=256, pm=256, ta=128, tb=64, tc=32, oa=2048, bh=512, bl=512, ab=128 * PE_SC).items():
+        _BF[_n + _f] = _w
+PACK = {}
+for _buf, _ty, _d in (("pint", "int32", _INT), ("pflt", "float32", _FLT), ("pbf", "bfloat16", _BF), ("pu", "uint16", _U16)):
+    _o = 0
+    for _n, _w in _d.items():
+        PACK[_n] = (_buf, _o, _w)
+        _o += _w
+    SCRATCH[_buf] = ("sbuf", [128, _o], _ty)
+SEMAPHORES = ["v", "a", "t", "p", "dx", "dm", "dt", "dy1", "dy2", "do",
+              "s1", "s2", "s3", "s4", "g1", "g2", "g3", "c", "r1", "r2", "r3", "col", "sg"]
+
+
+def layout(T, topo):
+    chips = []
+    for c in T.cores:
+        if topo.chip(c) not in chips:
+            chips.append(topo.chip(c))
+    nch = topo.chip(NC - 1) + 1
+    ranks = [[c for c in T.cores if topo.chip(c) == x] for x in chips]
+    on = {x: [c for c in range(NC) if topo.chip(c) == x] for x in range(nch)}
+    mate = [[x for x in range(nch) if topo.mates(ch, x)][0] for ch in chips]
+    n = len(chips)
+    same = [[d for d in range(n) if d != i and topo.same_plane(chips[i], chips[d])] for i in range(n)]
+    opp = [[d for d in range(n) if d != i and d not in same[i]] for i in range(n)]
+    helpers = [[c for c in on[chips[i]] if topo.die(c) != topo.die(ranks[i][0])] for i in range(n)]
+    hm = [[c for c in helpers[i] if topo.may_write(c, ranks[opp[i][0]][0])] for i in range(n)]
+    hs = [[c for c in helpers[i] if c not in hm[i]] for i in range(n)]
+    rel = [[c for c in on[mate[i]] if topo.may_write(c, ranks[i][0])] for i in range(n)]
+    gate, relay = {}, {}
+    for i in range(n):
+        for d in range(n):
+            if d == i:
+                continue
+            if d in same[i]:
+                for ph in (1, 2, 3):
+                    gate[ph, i, d] = hs[i][1 if ph == 2 else 0]
+                for k in range(4):
+                    relay[i, k, d] = helpers[i][k]
+            else:
+                w = opp[d].index(i)
+                gate[1, i, d] = hm[i][opp[i].index(d)]
+                gate[2, i, d] = rel[d][w]
+                gate[3, i, d] = rel[d][2 + w]
+                cant = [k for k in range(4) if not topo.may_write(ranks[i][k], ranks[d][0])]
+                for k in range(4):
+                    relay[i, k, d] = rel[d][2 * w + cant.index(k)] if k in cant else None
+    return ranks, same, opp, gate, relay
+
+
+def bits(m):
+    return [b for b in range(m.bit_length()) if (m >> b) & 1]
+
+
+def rank_program(g, core, T, topo):
+    ranks, same, opp, gate, relay = layout(T, topo)
+    n = len(ranks)
+    total = {}
+
+    def fused(moves, local):
+        used, out = [], {}
+        order = sorted(range(len(moves)), key=lambda j: len(bits(topo.mask(core, moves[j][2][0]))))
+        for j in order:
+            src, dst, dsts, ne, sem = moves[j]
+            free = [b for b in bits(topo.mask(core, dsts[0])) if b not in used]
+            leaves = topo.chip(dsts[0]) != topo.chip(core)
+            take = free[:ne] if leaves else free[len(free) - ne:]
+            used.extend(take)
+            ids = []
+            for c in dsts:
+                rid, pid, _e = topo.addr(c)
+                ids.append(DstId(rid=rid, pnc=pid))
+            out[j] = RemoteDMATransfer(dst_ids=ids, dma_engine_mask=sum(1 << b for b in take), remote_sem=T.sem[sem],
+                                       srcs=[src], dsts=[dst] * len(dsts))
+            total[local] = total.get(local, 0) + ne
+        g.remote_dma_fused([out[j] for j in range(len(moves))], local_sem=T.sem[local])
+
+    rank = T.rank_of(core)
+    if rank is None:
+        for ph in (1, 2, 3):
+            for i in range(n):
+                for d in range(n):
+                    if d != i and gate[ph, i, d] == core:
+                        g.wait_ge(T.sem["g%d" % ph], 4 * 4)
+                        fused([(T["gw%d" % ph][:], T["l%d" % ph][:, 32 * i:32 * i + 32], ranks[d], 8, "r%d" % ph)], "sg")
+        for i in range(n):
+            for d in range(n):
+                for k in range(4):
+                    if d != i and relay[i, k, d] == core:
+                        o = 4 * i + k
+                        g.wait_ge(T.sem.c, 8)
+                        fused([(T.rel[:, 256 * j:256 * j + 256], T.recv[:, 256 * o:256 * o + 256], [ranks[d][j]], 2, "col")
+                               for j in range(4)], "sg")
+        if "sg" in total:
+            g.wait_ge(T.sem.sg, total["sg"])
+        return
+
+    ci, ck = rank // 4, rank % 4
+    que = {"v": g.vector, "a": g.scalar, "t": g.tensor, "p": g, "s": g.sync}
+    seen = {}
+
+    def S(name, a=0, b=None, st=1):
+        buf, o, w = PACK[name]
+        hi = o + (w if b is None else b)
+        return T[buf][:, o + a:hi] if st == 1 else T[buf][:, o + a:hi:st]
+
+    def wait(q, deps):
+        for s, c in deps:
+            if seen.get((q, s), 0) < c:
+                que[q].wait_ge(T.sem[s], c)
+                seen[q, s] = c
+
+    def done(q, ins):
+        total[q] = total.get(q, 0) + 1
+        ins.then_inc(T.sem[q], 1)
+        return (q, total[q])
+
+    def ts(deps, out, in0, s1, s2, op0, op1=None):
+        wait("v", deps)
+        if op1 is None:
+            return done("v", g.vector.tensor_scalar(out, in0, s1, s2, op0))
+        return done("v", g.vector.tensor_scalar(out, in0, s1, s2, op0, op1))
+
+    def tt(deps, out, a, b, op):
+        wait("v", deps)
+        return done("v", g.vector.tensor_tensor(out, a, b, op))
+
+    def cp(deps, out, a):
+        wait("v", deps)
+        return done("v", g.vector.tensor_copy(out, a))
+
+    def scan(deps, out, a, b):
+        wait("v", deps)
+        return done("v", g.vector.tensor_tensor_scan(out, a, b, 0.0, OP.mult, OP.add))
+
+    def mm(deps, out, l, r, start=True, stop=True):
+        wait("t", deps)
+        return done("t", g.tensor.matmul(out, l, r, start, stop))
+
+    def act(deps, out, a, f, **kw):
+        wait("a", deps)
+        return done("a", g.scalar.activation(out, a, f, **kw))
+
+    def iota(out, pattern, base, cm):
+        return done("p", g.iota(out, pattern, base, cm, allow_small_or_imprecise_dtypes=True))
+
+    def dma(deps, out, in_, sem):
+        wait("s", deps)
+        g.sync.dma_start(out, in_).then_inc(T.sem[sem], 16)
+        total[sem] = total.get(sem, 0) + 16
+        return (sem, total[sem])
+
+    dx = dma([], T.x[:], T.idx[:], "dx")
+
+    def load_map(h):
+        for a in range(4):
+            p = 32 * a + 16 * h
+            r = dma([], T.win[p:p + 16, :], T.mp[:, 8192 * h:8192 * h + 8192], "dm")
+        return r
+
+    def load_tab(lo, hi):
+        for j in range(lo, hi):
+            r = dma([], T.tabs[:, 4096 * j:4096 * j + 4096], T.tab[:, 4096 * j:4096 * j + 4096], "dt")
+        return r
+    load_map(0)
+
+    k_ip = iota(S("ip"), [[0, 16]], 0, 1)
+    k_io = iota(S("iom"), [[1, 128]], 0, 0)
+    k_op = iota(S("opat"), [[1, 16], [0, 16]], 0, 0)
+    k_tp = iota(S("tpat"), [[0, 16], [1, 16]], 0, 0)
+    k_key = [iota(S("key", 128 * u, 128 * u + 128), [[32, 4], [0, 2], [1, 16]], 16 * u, 0) for u in (0, 1)]
+    k_b32 = iota(S("b32"), [[32, 32]], 0, 0)
+    k_lp = iota(S("lpat"), [[0, 32], [1, 16]], 0, 0)
+    k_k8 = iota(S("key8"), [[16, 8], [0, 8], [1, 16]], 0, 0)
+    t1 = ts([k_ip], S("ip15"), S("ip"), 15, None, OP.bitwise_and)
+    c_pc = cp([], S("pcol"), S("ip"))
+    c_of = cp([t1], S("offt"), S("ip15"))
+    c_p16 = cp([], S("p16"), S("ip15"))
+    pcol = S("pcol", 0, 1)
+    c_low = ts([k_io, c_pc], S("low"), S("iom"), pcol, None, OP.is_gt)
+    c_id = ts([], S("ident"), S("iom"), pcol, None, OP.is_equal)
+    c_d0 = ts([k_tp], S("d0"), S("tpat"), 1.0, None, OP.min)
+
+    def prep(f, x, dep, sh):
+        a = ts(dep, S("ow2" + f), x, sh + 2, None, OP.logical_shift_right)
+        pb = sh // 2
+        b = ts([], S("hh" + f), x, pb, (1 << pb) - 1, OP.logical_shift_right, OP.bitwise_and)
+        c = ts([], S("ll" + f), x, (1 << pb) - 1, None, OP.bitwise_and)
+        d = ts([a], S("cb4" + f), S("ow2" + f), 4.0, None, OP.mult)
+        z = -256.0 if f == "1" else 0.0
+        e = ts([b], S("vh" + f), S("hh" + f), z, float(1 << pb), OP.add, OP.mult)
+        h = ts([c], S("vl" + f), S("ll" + f), z, None, OP.add)
+        c2 = tt([d], S("cb" + f), S("cb4" + f), S("own" + f), OP.add)
+        return [c2, e, h]
+
+    def slots(f, x, dep, sh):
+        a = ts(dep, S("own" + f), x, sh, None, OP.logical_shift_right)
+        b = tt([a, c_of, k_op], S("oh" + f), S("own" + f).indirect(S("offt")), S("opat"), OP.is_equal)
+        c = scan([b, c_d0], S("s1" + f), S("d0"), S("oh" + f))
+        d = mm([c, c_low], T.psb[:, 0:16], S("low"), S("s1" + f, 15, 256, 16))
+        ohb0 = S("ohb" + f, 0, 256, 16)
+        e = cp([], S("ohb" + f), S("oh" + f))
+        h = ts([e], ohb0, S("oh" + f, 0, 256, 16), -1.0, None, OP.add)
+        pre = prep(f, x, [], sh)
+        i = tt([d, h], ohb0, ohb0, T.psb[:, 0:16], OP.add)
+        j = scan([i], S("cc" + f), S("d0"), S("ohb" + f))
+        k = tt([j], S("pm" + f), S("oh" + f), S("cc" + f), OP.mult)
+        k = tt([k], S("ta" + f), S("pm" + f, 0, 128), S("pm" + f, 128, 256), OP.add)
+        k = tt([k], S("tb" + f), S("ta" + f, 0, 64), S("ta" + f, 64, 128), OP.add)
+        k = tt([k], S("tc" + f), S("tb" + f, 0, 32), S("tb" + f, 32, 64), OP.add)
+        k = tt([k], S("rk" + f), S("tc" + f, 0, 16), S("tc" + f, 16, 32), OP.add)
+        gm = ts([k], S("gm" + f), S("rk" + f), 128.0, -128.0, OP.is_ge, OP.mult)
+        g4 = ts([], S("ge4" + f), S("rk" + f), 128.0, 4.0, OP.is_ge, OP.mult)
+        lo = tt([gm], S("lo" + f), S("gm" + f), S("rk" + f), OP.add)
+        hi = tt([g4, pre[0]], S("hi" + f), S("ge4" + f), S("cb" + f), OP.add)
+        nl = ts([lo], S("nlo" + f), S("lo" + f), -1.0, None, OP.mult)
+        return lo, hi, nl, pre
+
+    def compact(f, lo, hi, nl, pre):
+        tok = {}
+        for z in range(PE_SC):
+            t = 16 - PE_SC + z
+            ab = S("ab" + f, 128 * z, 128 * z + 128)
+            a = act([nl, k_io], ab, S("iom"), AF.Abs, bias=S("nlo" + f, t, t + 1))
+            tok[t] = act([a], S("oa" + f, 128 * t, 128 * t + 128), ab, AF.Relu, bias=1.0, scale=-1.0)
+        io32 = S("iom", 0, 32)
+        for t in range(16):
+            oa, bh, bl = S("oa" + f, 128 * t, 128 * t + 128), S("bh" + f, 32 * t, 32 * t + 32), S("bl" + f, 32 * t, 32 * t + 32)
+            ta = [tok[t]] if t in tok else [ts([lo], oa, S("iom"), S("lo" + f, t, t + 1), None, OP.is_equal)]
+            th = ts([hi] + pre, bh, io32, S("hi" + f, t, t + 1), S("vh" + f, t, t + 1), OP.is_equal, OP.mult)
+            tl = ts([], bl, io32, S("hi" + f, t, t + 1), S("vl" + f, t, t + 1), OP.is_equal, OP.mult)
+            mm(ta + [th], T.pse[:, 0:32], oa, bh, t == 0, False)
+            r = mm([tl], T.pse[:, 0:32], oa, bl, False, t == 15)
+        return r
+
+    def spread(ph, q, dep):
+        land = T["l%d" % ph]
+        sib = [c for c in ranks[ci] if c != core]
+        moves = [(q[:, 8 * d:8 * d + 8], T["gw%d" % ph][:, 8 * ck:8 * ck + 8], [gate[ph, ci, d]], 4, "g%d" % ph)
+                 for d in opp[ci] + same[ci]]
+        moves.append((q[:, 8 * ci:8 * ci + 8], land[:, 8 * rank:8 * rank + 8], sib, 4, "r%d" % ph))
+        wait("p", [dep])
+        fused(moves, "s%d" % ph)
+        total["r%d" % ph] = 4 * len(sib) + 8 * (n - 1)
+        return [cp([dep], land[:, 8 * rank:8 * rank + 8], q[:, 8 * ci:8 * ci + 8]), ("r%d" % ph, total["r%d" % ph])]
+
+    lo, hi, nl, pre = slots("1", T.x[:], [dx], MSH)
+    r = compact("1", lo, hi, nl, pre)
+    q = ts([r], T.q1[:], T.pse[:, 0:32], BIAS, None, OP.add)
+    got1 = spread(1, T.q1, q)
+    wait("s", [("s1", total["s1"])])
+    dm = load_map(1)
+    load_tab(0, 2)
+    tr = []
+    for t in range(16):
+        wait("t", [c_id])
+        tr.append(done("t", g.tensor.transpose(T.pst[:, 128 * t:128 * t + 128], S("oa1", 128 * t, 128 * t + 128), S("ident"))))
+    c_at = [act([tr[8 * h + 7]], S("at", 1024 * h, 1024 * h + 1024), T.pst[:, 1024 * h:1024 * h + 1024], AF.Copy) for h in (0, 1)]
+    c_su = [ts([k_key[u]], S("su", 128 * u, 128 * u + 128), S("key", 128 * u, 128 * u + 128), pcol, None, OP.is_equal)
+            for u in (0, 1)]
+    c_dm = ts([k_lp, c_p16], S("dmask"), S("lpat"), S("p16", 0, 1), None, OP.is_equal)
+    a = ts([], S("g16"), S("rk1"), 128.0, 16.0, OP.is_ge, OP.mult)
+    a = tt([a], S("hi01"), S("g16"), S("own1"), OP.add)
+    for t in range(16):
+        c_b01 = ts([a], S("b01", 32 * t, 32 * t + 32), S("iom", 0, 32), S("hi01", t, t + 1), None, OP.is_equal)
+    c_s8 = ts([k_k8], S("s8"), S("key8"), pcol, None, OP.is_equal)
+
+    mine = T.l1[:, ck::4]
+    a = ts(got1, S("ci"), mine, 4, 8191, OP.logical_shift_right, OP.bitwise_and)
+    b = cp([a], S("cf"), S("ci"))
+    for u in (0, 1):
+        d = mm([b, c_su[u]], T.psd[:, u:64:2], S("su", 128 * u, 128 * u + 128), S("cf"))
+    y1 = ts([], S("yq"), mine, 15, None, OP.bitwise_and)
+    y2 = ts([], S("yh"), mine, 13, 16, OP.logical_shift_right, OP.bitwise_and)
+    y3 = tt([y1, k_b32], S("ya"), S("yq"), S("b32"), OP.add)
+    y4 = tt([y3, y2], S("yb"), S("ya"), S("yh"), OP.add)
+    e = cp([d], S("coff"), T.psd[:, 0:64])
+    y5 = cp([y4], S("o2"), S("yb"))
+    a = cp([e, dm], S("gat"), T.win[:, 0:8192].indirect(S("coff")))
+    wait("v", [a])
+    a = done("v", g.vector.transpose(S("gt"), S("gat")))
+    a = tt([a, y5, c_dm], S("ff"), S("gt").indirect(S("o2")), S("dmask"), OP.mult)
+    a = tt([a], S("f1"), S("ff", 0, 512, 2), S("ff", 1, 512, 2), OP.add)
+    a = tt([a], S("f2"), S("f1", 0, 256, 2), S("f1", 1, 256, 2), OP.add)
+    a = tt([a], S("f3"), S("f2", 0, 128, 2), S("f2", 1, 128, 2), OP.add)
+    a = tt([a], T.q2[:], S("f3", 0, 64, 2), S("f3", 1, 64, 2), OP.add)
+    got2 = spread(2, T.q2, a)
+    wait("s", [("s2", total["s2"])])
+    dt = load_tab(2, 4)
+
+    hs, ls = [], []
+    for k in (0, 1):
+        src = T.l2[:, 2 * ck + k::8]
+        hs.append(ts(got2, S("mh", 16 * k, 16 * k + 16), src, 9, None, OP.logical_shift_right))
+        ls.append(ts([], S("ml", 16 * k, 16 * k + 16), src, 511, None, OP.bitwise_and))
+    hb = ts(hs, S("hb"), S("mh"), -256.0, 512.0, OP.add, OP.mult)
+    lb = ts(ls, S("lb"), S("ml"), -256.0, None, OP.add)
+    sums = []
+    for h in (0, 1):
+        ps = T["psu%d" % h]
+        for t in range(8):
+            w = S("at", 1024 * h + 128 * t, 1024 * h + 128 * t + 128)
+            mm([hb, c_at[h]], ps[:, 32 * t:32 * t + 32], w, S("hb"), True, False)
+            r = mm([lb], ps[:, 32 * t:32 * t + 32], w, S("lb"), False, True)
+        pr = tt([r, c_b01], S("pr", 256 * h, 256 * h + 256), ps[:, 0:256], S("b01", 256 * h, 256 * h + 256), OP.mult)
+        for t in range(8):
+            c0, col = 256 * h + 32 * t, 8 * h + t
+            if t < 5:
+                wait("v", [pr])
+                sums.append(done("v", g.vector.tensor_reduce(S("mf", col, col + 1), S("pr", c0, c0 + 32), AxisListType.X, OP.add)))
+            else:
+                sums.append(act([pr], S("junk", c0, c0 + 32), S("pr", c0, c0 + 32), AF.Copy, accum_out=S("mf", col, col + 1)))
+    m = ts(sums, S("m"), S("mf"), BIAS, None, OP.add)
+
+    lo, hi, nl, pre = slots("2", S("m"), [m], TSH)
+    r = compact("2", lo, hi, nl, pre)
+    q = cp([r], T.q3[:], T.pse[:, 0:32])
+    got3 = spread(3, T.q3, q)
+    a = ts([], S("o256"), S("own2"), 256.0, None, OP.mult)
+    a = tt([a], S("sl"), S("o256"), S("rk2"), OP.add)
+    a = cp([a], T.slu[:], S("sl"))
+    a = dma([a], T.ysl[:], T.slu[:], "dy1")
+    for j in range(8):
+        yo = dma([a], T.yoff[16 * j:16 * j + 16, :], T.ysl[:], "dy2")
+
+    for pg in range(8):
+        r = mm(got3 + [c_s8], T.psf[:, pg:256:8], S("s8", 128 * pg, 128 * pg + 128), T.l3[:, ck::4])
+    of = cp([r], S("off"), T.psf[:, 0:256])
+
+    def gather(eng, c0, c1, out):
+        src = T.tabs[:, 0:16384].indirect(S("off", c0, c1))
+        if eng == "v":
+            return cp([of, dt], out, src)
+        return act([of, dt], out, src, AF.Copy)
+
+    o = rank
+    mine_tok = []
+    for d in (opp[ci][0], same[ci][0], opp[ci][1], ci):
+        if d != ci:
+            c0 = 64 * d
+            tv = gather("v", c0, c0 + 32, T.gout[:, 16 * c0:16 * c0 + 512])
+            ta = gather("a", c0 + 32, c0 + 64, T.gout[:, 16 * c0 + 512:16 * c0 + 1024])
+            wait("p", [tv, ta])
+            via = relay[ci, ck, d]
+            if via is not None:
+                fused([(T.gout[:, 1024 * d:1024 * d + 1024], T.rel[:], [via], 8, "c")], "s4")
+            else:
+                fused([(T.gout[:, 1024 * d + 256 * j:1024 * d + 256 * j + 256], T.recv[:, 256 * o:256 * o + 256],
+                        [ranks[d][j]], 2, "col") for j in range(4)], "s4")
+        else:
+            toks = []
+            for j in range(4):
+                c0 = 64 * d + 16 * j
+                dst = T.recv[:, 256 * o:256 * o + 256] if j == ck else T.gout[:, 16 * c0:16 * c0 + 256]
+                tk = gather("v" if j % 2 == 0 else "a", c0, c0 + 16, dst)
+                if j == ck:
+                    mine_tok.append(tk)
+                else:
+                    toks.append(tk)
+            wait("p", toks)
+            fused([(T.gout[:, 1024 * d + 256 * j:1024 * d + 256 * j + 256], T.recv[:, 256 * o:256 * o + 256],
+                    [ranks[d][j]], 4, "col") for j in range(4) if j != ck], "s4")
+    total["col"] = 3 * 4 + 12 * 2
+
+    arrived = mine_tok + [("col", total["col"]), yo]
+    for j in range(4):
+        src = T.recv[:, 0:4096].indirect(T.yoff[:, 32 * j:32 * j + 32])
+        out = T.ys[:, 512 * j:512 * j + 512]
+        tk = cp(arrived, out, src) if j % 2 == 0 else act(arrived, out, src, AF.Copy)
+        dma([tk], T.y[:, 512 * j:512 * j + 512], out, "do")
+    wait("p", [(s, total[s]) for s in total])

@@ -4,30 +4,30 @@ from concourse.mybir import AluOpType as OP, AxisListType, ActivationFunctionTyp
 NC = 112
 MSH, TSH = 18, 14
 BIAS = float((1 << 17) + 256)
-PE_SC = 5
+BY_S = 12
 
 SCRATCH = {
     "x": ("sbuf", [128, 16], "int32"), "win": ("sbuf", [128, 8192], "int32"), "tabs": ("sbuf", [128, 16384], "bfloat16"),
     "recv": ("sbuf", [128, 4096], "bfloat16"), "gout": ("sbuf", [128, 4096], "bfloat16"), "ys": ("sbuf", [128, 2048], "bfloat16"),
     "rel": ("sbuf", [128, 1024], "bfloat16"), "slu": ("sbuf", [128, 16], "uint16"), "yoff": ("sbuf", [128, 128], "uint16"),
     "ysl": ("dram", [16, 128], "uint16"), "pst": ("psum", [128, 2048], "bfloat16"),
-    "q1": ("sbuf", [128, 32], "int32"), "q2": ("sbuf", [128, 32], "int32"), "q3": ("sbuf", [128, 32], "float32"),
-    "gw1": ("sbuf", [128, 32], "int32"), "gw2": ("sbuf", [128, 32], "int32"), "gw3": ("sbuf", [128, 32], "float32"),
-    "l1": ("sbuf", [128, 128], "int32"), "l2": ("sbuf", [128, 128], "int32"), "l3": ("sbuf", [128, 128], "float32"),
+    "q1": ("sbuf", [128, 32], "int32"), "q2": ("sbuf", [128, 32], "int32"), "q3": ("sbuf", [128, 64], "bfloat16"),
+    "gw1": ("sbuf", [128, 32], "int32"), "gw2": ("sbuf", [128, 32], "int32"), "gw3": ("sbuf", [128, 64], "bfloat16"),
+    "l1": ("sbuf", [128, 128], "int32"), "l2": ("sbuf", [128, 128], "int32"), "l3": ("sbuf", [128, 256], "bfloat16"),
 }
 for _n in ("psb", "pse", "psu0", "psu1", "psd", "psf"):
     SCRATCH[_n] = ("psum", [128, 512], "float32")
 _INT = dict(ip=16, ip15=16, b32=32, ci=32, yq=32, yh=32, ya=32, yb=32, mh=32, ml=32, m=16)
-_FLT = dict(pcol=16, p16=16, key=256, su=256, key8=1024, s8=1024, lpat=512, dmask=512, g16=16, hi01=16, cf=32, gat=1024, gt=1024,
-            ff=512, f1=256, f2=128, f3=64, pr=512, junk=512, mf=16, o256=16, sl=16)
-_BF = dict(iom=128, opat=256, tpat=256, d0=256, low=128, ident=128, at=2048, b01=512, hb=32, lb=32)
+_FLT = dict(pcol=16, p16=16, key=256, su=256, lpat=512, dmask=512, cf=32, gat=1024, gt=1024,
+            ff=512, f1=512, pr=512, junk=512, mf=16, o256=16, sl=16)
+_BF = dict(iom1=128, io0=32, io32p=32, opat=256, d0=512, low=128, ident=128, at=2048, b01=512, hb=32, lb=32, key8=1024, s8=1024)
 _U16 = dict(offt=16, coff=64, o2=32, off=256)
 for _f in "12":
-    for _n in ("own", "ow2", "hh", "ll"):
+    for _n in ("own", "hh", "ll"):
         _INT[_n + _f] = 16
-    for _n in ("cb4", "cb", "vh", "vl", "rk", "ge4", "gm", "hi", "lo", "nlo"):
+    for _n in ("vh", "vl", "rk", "g16", "gm", "hi", "lo"):
         _FLT[_n + _f] = 16
-    for _n, _w in dict(oh=256, s1=256, ohb=256, cc=256, pm=256, ta=128, tb=64, tc=32, oa=2048, bh=512, bl=512, ab=128 * PE_SC).items():
+    for _n, _w in dict(oh=256, s1=256, ohb=256, cc=256, pm=128, ta=128, tb=64, tc=32, oa=2048, bb=1024, bo=512).items():
         _BF[_n + _f] = _w
 PACK = {}
 for _buf, _ty, _d in (("pint", "int32", _INT), ("pflt", "float32", _FLT), ("pbf", "bfloat16", _BF), ("pu", "uint16", _U16)):
@@ -36,8 +36,8 @@ for _buf, _ty, _d in (("pint", "int32", _INT), ("pflt", "float32", _FLT), ("pbf"
         PACK[_n] = (_buf, _o, _w)
         _o += _w
     SCRATCH[_buf] = ("sbuf", [128, _o], _ty)
-SEMAPHORES = ["v", "a", "t", "p", "dx", "dm", "dt", "dy1", "dy2", "do",
-              "s1", "s2", "s3", "s4", "g1", "g2", "g3", "c", "r1", "r2", "r3", "col", "sg"]
+SEMAPHORES = ["v", "a", "t", "p", "dx", "dm", "dt", "dy1", "dy2", "do", "i1", "i2",
+              "s1", "s2", "s3", "s4", "g1", "g2", "g3", "c0", "c1", "r1", "r2", "r3", "col", "sg"]
 
 
 def layout(T, topo):
@@ -61,18 +61,16 @@ def layout(T, topo):
         for d in range(n):
             if d == i:
                 continue
-            if d in same[i]:
-                for ph in (1, 2, 3):
-                    gate[ph, i, d] = hs[i][1 if ph == 2 else 0]
-                for k in range(4):
-                    relay[i, k, d] = helpers[i][k]
-            else:
-                w = opp[d].index(i)
-                gate[1, i, d] = hm[i][opp[i].index(d)]
-                gate[2, i, d] = rel[d][w]
-                gate[3, i, d] = rel[d][2 + w]
-                cant = [k for k in range(4) if not topo.may_write(ranks[i][k], ranks[d][0])]
-                for k in range(4):
+            w = opp[d].index(i) if d in opp[i] else None
+            cant = [k for k in range(4) if not topo.may_write(ranks[i][k], ranks[d][0])]
+            for k in range(4):
+                if w is None:
+                    gate[1, i, k, d] = relay[i, k, d] = helpers[i][k]
+                    gate[2, i, k, d] = hs[i][0]
+                    gate[3, i, k, d] = hs[i][1]
+                else:
+                    gate[1, i, k, d] = rel[d][2 * w + k // 2]
+                    gate[2, i, k, d] = gate[3, i, k, d] = hm[i][opp[i].index(d)]
                     relay[i, k, d] = rel[d][2 * w + cant.index(k)] if k in cant else None
     return ranks, same, opp, gate, relay
 
@@ -85,6 +83,7 @@ def rank_program(g, core, T, topo):
     ranks, same, opp, gate, relay = layout(T, topo)
     n = len(ranks)
     total = {}
+    blk = {1: 8, 2: 8, 3: 16}
 
     def fused(moves, local):
         used, out = [], {}
@@ -104,22 +103,34 @@ def rank_program(g, core, T, topo):
             total[local] = total.get(local, 0) + ne
         g.remote_dma_fused([out[j] for j in range(len(moves))], local_sem=T.sem[local])
 
+    def hop1(i, d):
+        return 8 if d in same[i] else 4
+
+    def pieces(i, k, d):
+        return [(0, 512), (512, 1024)] if d == opp[i][1] else [(0, 1024)]
+
     rank = T.rank_of(core)
     if rank is None:
         for ph in (1, 2, 3):
+            w = blk[ph]
             for i in range(n):
                 for d in range(n):
-                    if d != i and gate[ph, i, d] == core:
-                        g.wait_ge(T.sem["g%d" % ph], 4 * 4)
-                        fused([(T["gw%d" % ph][:], T["l%d" % ph][:, 32 * i:32 * i + 32], ranks[d], 8, "r%d" % ph)], "sg")
+                    ks = [k for k in range(4) if d != i and gate[ph, i, k, d] == core]
+                    if ks:
+                        g.wait_ge(T.sem["g%d" % ph], hop1(i, d) * len(ks))
+                        a = w * (4 * i + ks[0])
+                        fused([(T["gw%d" % ph][:, 0:w * len(ks)], T["l%d" % ph][:, a:a + w * len(ks)], ranks[d], 8, "r%d" % ph)],
+                              "sg")
         for i in range(n):
             for d in range(n):
                 for k in range(4):
                     if d != i and relay[i, k, d] == core:
                         o = 4 * i + k
-                        g.wait_ge(T.sem.c, 8)
-                        fused([(T.rel[:, 256 * j:256 * j + 256], T.recv[:, 256 * o:256 * o + 256], [ranks[d][j]], 2, "col")
-                               for j in range(4)], "sg")
+                        for z, (a, b) in enumerate(pieces(i, k, d)):
+                            g.wait_ge(T.sem["c%d" % z], 8)
+                            js = range(a // 256, b // 256)
+                            fused([(T.rel[:, 256 * j:256 * j + 256], T.recv[:, 256 * o:256 * o + 256], [ranks[d][j]],
+                                    8 // len(js), "col") for j in js], "sg")
         if "sg" in total:
             g.wait_ge(T.sem.sg, total["sg"])
         return
@@ -158,6 +169,10 @@ def rank_program(g, core, T, topo):
         wait("v", deps)
         return done("v", g.vector.tensor_copy(out, a))
 
+    def fill(deps, out, c):
+        wait("v", deps)
+        return done("v", g.vector.memset(out, c))
+
     def scan(deps, out, a, b):
         wait("v", deps)
         return done("v", g.vector.tensor_tensor_scan(out, a, b, 0.0, OP.mult, OP.add))
@@ -181,8 +196,9 @@ def rank_program(g, core, T, topo):
 
     dx = dma([], T.x[:], T.idx[:], "dx")
 
-    def load_map(h):
-        for a in range(4):
+    def load_map(lo, hi):
+        for j in range(lo, hi):
+            h, a = j // 4, j % 4
             p = 32 * a + 16 * h
             r = dma([], T.win[p:p + 16, :], T.mp[:, 8192 * h:8192 * h + 8192], "dm")
         return r
@@ -191,94 +207,99 @@ def rank_program(g, core, T, topo):
         for j in range(lo, hi):
             r = dma([], T.tabs[:, 4096 * j:4096 * j + 4096], T.tab[:, 4096 * j:4096 * j + 4096], "dt")
         return r
-    load_map(0)
+    load_map(0, 6)
 
     k_ip = iota(S("ip"), [[0, 16]], 0, 1)
-    k_io = iota(S("iom"), [[1, 128]], 0, 0)
     k_op = iota(S("opat"), [[1, 16], [0, 16]], 0, 0)
-    k_tp = iota(S("tpat"), [[0, 16], [1, 16]], 0, 0)
-    k_key = [iota(S("key", 128 * u, 128 * u + 128), [[32, 4], [0, 2], [1, 16]], 16 * u, 0) for u in (0, 1)]
+    k_io = iota(S("iom1"), [[1, 128]], 1, 0)
+    k_ipp = iota(S("io32p"), [[4, 4], [16, 2], [1, 4]], 0, 0)
+    k_io0 = iota(S("io0"), [[1, 32]], 0, 0)
+    k_key = [iota(S("key", 128 * u, 128 * u + 128), [[32, 4], [0, 2], [1, 16]], 16 * u + 1, 0) for u in (0, 1)]
     k_b32 = iota(S("b32"), [[32, 32]], 0, 0)
     k_lp = iota(S("lpat"), [[0, 32], [1, 16]], 0, 0)
-    k_k8 = iota(S("key8"), [[16, 8], [0, 8], [1, 16]], 0, 0)
+    k_k8 = iota(S("key8"), [[16, 8], [0, 8], [1, 16]], 1, 0)
+    c = fill([], S("d0"), 1.0)
+    c_d0 = fill([c], S("d0", 0, 512, 16), 0.0)
     t1 = ts([k_ip], S("ip15"), S("ip"), 15, None, OP.bitwise_and)
-    c_pc = cp([], S("pcol"), S("ip"))
+    c_pc = ts([], S("pcol"), S("ip"), 1.0, None, OP.add)
     c_of = cp([t1], S("offt"), S("ip15"))
     c_p16 = cp([], S("p16"), S("ip15"))
     pcol = S("pcol", 0, 1)
-    c_low = ts([k_io, c_pc], S("low"), S("iom"), pcol, None, OP.is_gt)
-    c_id = ts([], S("ident"), S("iom"), pcol, None, OP.is_equal)
-    c_d0 = ts([k_tp], S("d0"), S("tpat"), 1.0, None, OP.min)
-
-    def prep(f, x, dep, sh):
-        a = ts(dep, S("ow2" + f), x, sh + 2, None, OP.logical_shift_right)
-        pb = sh // 2
-        b = ts([], S("hh" + f), x, pb, (1 << pb) - 1, OP.logical_shift_right, OP.bitwise_and)
-        c = ts([], S("ll" + f), x, (1 << pb) - 1, None, OP.bitwise_and)
-        d = ts([a], S("cb4" + f), S("ow2" + f), 4.0, None, OP.mult)
-        z = -256.0 if f == "1" else 0.0
-        e = ts([b], S("vh" + f), S("hh" + f), z, float(1 << pb), OP.add, OP.mult)
-        h = ts([c], S("vl" + f), S("ll" + f), z, None, OP.add)
-        c2 = tt([d], S("cb" + f), S("cb4" + f), S("own" + f), OP.add)
-        return [c2, e, h]
+    c_low = ts([k_io, c_pc], S("low"), S("iom1"), pcol, None, OP.is_gt)
+    c_id = ts([], S("ident"), S("iom1"), pcol, None, OP.is_equal)
 
     def slots(f, x, dep, sh):
         a = ts(dep, S("own" + f), x, sh, None, OP.logical_shift_right)
         b = tt([a, c_of, k_op], S("oh" + f), S("own" + f).indirect(S("offt")), S("opat"), OP.is_equal)
-        c = scan([b, c_d0], S("s1" + f), S("d0"), S("oh" + f))
+        ohp = act([b], T.psu0[:, 0:256], S("oh" + f), AF.Copy)
+        c = scan([b, c_d0], S("s1" + f), S("d0", 0, 256), S("oh" + f))
         d = mm([c, c_low], T.psb[:, 0:16], S("low"), S("s1" + f, 15, 256, 16))
         ohb0 = S("ohb" + f, 0, 256, 16)
         e = cp([], S("ohb" + f), S("oh" + f))
-        h = ts([e], ohb0, S("oh" + f, 0, 256, 16), -1.0, None, OP.add)
-        pre = prep(f, x, [], sh)
-        i = tt([d, h], ohb0, ohb0, T.psb[:, 0:16], OP.add)
-        j = scan([i], S("cc" + f), S("d0"), S("ohb" + f))
-        k = tt([j], S("pm" + f), S("oh" + f), S("cc" + f), OP.mult)
-        k = tt([k], S("ta" + f), S("pm" + f, 0, 128), S("pm" + f, 128, 256), OP.add)
+        pb, z = sh // 2, (-256.0 if f == "1" else 0.0)
+        ph = ts([], S("hh" + f), x, pb, (1 << pb) - 1, OP.logical_shift_right, OP.bitwise_and)
+        pl = ts([], S("ll" + f), x, (1 << pb) - 1, None, OP.bitwise_and)
+        vh = ts([ph], S("vh" + f), S("hh" + f), z, float(1 << pb), OP.add, OP.mult)
+        vl = ts([pl], S("vl" + f), S("ll" + f), z, None, OP.add)
+        i = tt([d, e], ohb0, ohb0, T.psb[:, 0:16], OP.add)
+        j = scan([i], S("cc" + f), S("d0", 0, 256), S("ohb" + f))
+        tt([j, ohp], S("pm" + f), T.psu0[:, 0:128], S("cc" + f, 0, 128), OP.mult)
+        k = tt([], T.psu1[:, 0:128], T.psu0[:, 128:256], S("cc" + f, 128, 256), OP.mult)
+        k = tt([k], S("ta" + f), S("pm" + f), T.psu1[:, 0:128], OP.add)
         k = tt([k], S("tb" + f), S("ta" + f, 0, 64), S("ta" + f, 64, 128), OP.add)
         k = tt([k], S("tc" + f), S("tb" + f, 0, 32), S("tb" + f, 32, 64), OP.add)
         k = tt([k], S("rk" + f), S("tc" + f, 0, 16), S("tc" + f, 16, 32), OP.add)
-        gm = ts([k], S("gm" + f), S("rk" + f), 128.0, -128.0, OP.is_ge, OP.mult)
-        g4 = ts([], S("ge4" + f), S("rk" + f), 128.0, 4.0, OP.is_ge, OP.mult)
+        gm = ts([k], S("gm" + f), S("rk" + f), 129.0, -128.0, OP.is_ge, OP.mult)
+        g16 = ts([], S("g16" + f), S("rk" + f), 129.0, 16.0, OP.is_ge, OP.mult)
         lo = tt([gm], S("lo" + f), S("gm" + f), S("rk" + f), OP.add)
-        hi = tt([g4, pre[0]], S("hi" + f), S("ge4" + f), S("cb" + f), OP.add)
-        nl = ts([lo], S("nlo" + f), S("lo" + f), -1.0, None, OP.mult)
-        return lo, hi, nl, pre
+        hi = tt([g16], S("hi" + f), S("g16" + f), S("own" + f), OP.add)
+        return lo, hi, vh, vl
 
-    def compact(f, lo, hi, nl, pre):
-        tok = {}
-        for z in range(PE_SC):
-            t = 16 - PE_SC + z
-            ab = S("ab" + f, 128 * z, 128 * z + 128)
-            a = act([nl, k_io], ab, S("iom"), AF.Abs, bias=S("nlo" + f, t, t + 1))
-            tok[t] = act([a], S("oa" + f, 128 * t, 128 * t + 128), ab, AF.Relu, bias=1.0, scale=-1.0)
-        io32 = S("iom", 0, 32)
+    def compact(f, lo, hi, vh, vl):
         for t in range(16):
-            oa, bh, bl = S("oa" + f, 128 * t, 128 * t + 128), S("bh" + f, 32 * t, 32 * t + 32), S("bl" + f, 32 * t, 32 * t + 32)
-            ta = [tok[t]] if t in tok else [ts([lo], oa, S("iom"), S("lo" + f, t, t + 1), None, OP.is_equal)]
-            th = ts([hi] + pre, bh, io32, S("hi" + f, t, t + 1), S("vh" + f, t, t + 1), OP.is_equal, OP.mult)
-            tl = ts([], bl, io32, S("hi" + f, t, t + 1), S("vl" + f, t, t + 1), OP.is_equal, OP.mult)
-            mm(ta + [th], T.pse[:, 0:32], oa, bh, t == 0, False)
-            r = mm([tl], T.pse[:, 0:32], oa, bl, False, t == 15)
+            oa, bo = S("oa" + f, 128 * t, 128 * t + 128), S("bo" + f, 32 * t, 32 * t + 32)
+            bh, bl = S("bb" + f, 64 * t, 64 * t + 64, 2), S("bb" + f, 64 * t + 1, 64 * t + 64, 2)
+            h, ch, cl = S("hi" + f, t, t + 1), S("vh" + f, t, t + 1), S("vl" + f, t, t + 1)
+            if t < BY_S:
+                b = ts([hi, k_ipp], bo, S("io32p"), h, None, OP.is_equal)
+                ta = ts([lo], oa, S("iom1"), S("lo" + f, t, t + 1), None, OP.is_equal)
+                th = act([b, vh], bh, bo, AF.Copy, scale=ch)
+                tl = act([vl], bl, bo, AF.Copy, scale=cl)
+            else:
+                th = ts([hi, vh], bh, S("io32p"), h, ch, OP.is_equal, OP.mult)
+                tl = ts([vl], bl, S("io32p"), h, cl, OP.is_equal, OP.mult)
+                ta = ts([lo], oa, S("iom1"), S("lo" + f, t, t + 1), None, OP.is_equal)
+            if f == "1":
+                mm([ta, th], T.pse[:, 0:32], oa, bh, t == 0, False)
+                r = mm([tl], T.pse[:, 0:32], oa, bl, False, t == 15)
+            else:
+                r = mm([ta, th, tl], T.pse[:, 0:64], oa, S("bb" + f, 64 * t, 64 * t + 64), t == 0, t == 15)
         return r
 
     def spread(ph, q, dep):
-        land = T["l%d" % ph]
+        land, w = T["l%d" % ph], blk[ph]
         sib = [c for c in ranks[ci] if c != core]
-        moves = [(q[:, 8 * d:8 * d + 8], T["gw%d" % ph][:, 8 * ck:8 * ck + 8], [gate[ph, ci, d]], 4, "g%d" % ph)
-                 for d in opp[ci] + same[ci]]
-        moves.append((q[:, 8 * ci:8 * ci + 8], land[:, 8 * rank:8 * rank + 8], sib, 4, "r%d" % ph))
+        moves = []
+        for d in opp[ci] + same[ci]:
+            r = gate[ph, ci, ck, d]
+            a = w * (ck - min(k for k in range(4) if gate[ph, ci, k, d] == r))
+            moves.append((q[:, w * d:w * d + w], T["gw%d" % ph][:, a:a + w], [r], hop1(ci, d), "g%d" % ph))
         wait("p", [dep])
         fused(moves, "s%d" % ph)
-        total["r%d" % ph] = 4 * len(sib) + 8 * (n - 1)
-        return [cp([dep], land[:, 8 * rank:8 * rank + 8], q[:, 8 * ci:8 * ci + 8]), ("r%d" % ph, total["r%d" % ph])]
+        fused([(q[:, w * ci:w * ci + w], land[:, w * rank:w * rank + w], sib, 8, "r%d" % ph)], "s%d" % ph)
+        total["r%d" % ph] = 8 * len(sib) + 8 * sum(len(set(gate[ph, i, k, ci] for k in range(4))) for i in range(n) if i != ci)
+        return [cp([dep], land[:, w * rank:w * rank + w], q[:, w * ci:w * ci + w]), ("r%d" % ph, total["r%d" % ph])]
 
-    lo, hi, nl, pre = slots("1", T.x[:], [dx], MSH)
-    r = compact("1", lo, hi, nl, pre)
+    def issued(name):
+        g.sem_inc(T.sem[name], 1)
+        total[name] = 1
+        wait("s", [(name, 1)])
+
+    r = compact("1", *slots("1", T.x[:], [dx], MSH))
     q = ts([r], T.q1[:], T.pse[:, 0:32], BIAS, None, OP.add)
     got1 = spread(1, T.q1, q)
-    wait("s", [("s1", total["s1"])])
-    dm = load_map(1)
+    issued("i1")
+    dm = load_map(6, 8)
     load_tab(0, 2)
     tr = []
     for t in range(16):
@@ -288,10 +309,8 @@ def rank_program(g, core, T, topo):
     c_su = [ts([k_key[u]], S("su", 128 * u, 128 * u + 128), S("key", 128 * u, 128 * u + 128), pcol, None, OP.is_equal)
             for u in (0, 1)]
     c_dm = ts([k_lp, c_p16], S("dmask"), S("lpat"), S("p16", 0, 1), None, OP.is_equal)
-    a = ts([], S("g16"), S("rk1"), 128.0, 16.0, OP.is_ge, OP.mult)
-    a = tt([a], S("hi01"), S("g16"), S("own1"), OP.add)
     for t in range(16):
-        c_b01 = ts([a], S("b01", 32 * t, 32 * t + 32), S("iom", 0, 32), S("hi01", t, t + 1), None, OP.is_equal)
+        c_b01 = ts([k_io0], S("b01", 32 * t, 32 * t + 32), S("io0"), S("hi1", t, t + 1), None, OP.is_equal)
     c_s8 = ts([k_k8], S("s8"), S("key8"), pcol, None, OP.is_equal)
 
     mine = T.l1[:, ck::4]
@@ -309,12 +328,10 @@ def rank_program(g, core, T, topo):
     wait("v", [a])
     a = done("v", g.vector.transpose(S("gt"), S("gat")))
     a = tt([a, y5, c_dm], S("ff"), S("gt").indirect(S("o2")), S("dmask"), OP.mult)
-    a = tt([a], S("f1"), S("ff", 0, 512, 2), S("ff", 1, 512, 2), OP.add)
-    a = tt([a], S("f2"), S("f1", 0, 256, 2), S("f1", 1, 256, 2), OP.add)
-    a = tt([a], S("f3"), S("f2", 0, 128, 2), S("f2", 1, 128, 2), OP.add)
-    a = tt([a], T.q2[:], S("f3", 0, 64, 2), S("f3", 1, 64, 2), OP.add)
+    a = scan([a], S("f1"), S("d0"), S("ff"))
+    a = cp([a], T.q2[:], S("f1", 15, 512, 16))
     got2 = spread(2, T.q2, a)
-    wait("s", [("s2", total["s2"])])
+    issued("i2")
     dt = load_tab(2, 4)
 
     hs, ls = [], []
@@ -325,27 +342,26 @@ def rank_program(g, core, T, topo):
     hb = ts(hs, S("hb"), S("mh"), -256.0, 512.0, OP.add, OP.mult)
     lb = ts(ls, S("lb"), S("ml"), -256.0, None, OP.add)
     sums = []
-    for h in (0, 1):
-        ps = T["psu%d" % h]
-        for t in range(8):
-            w = S("at", 1024 * h + 128 * t, 1024 * h + 128 * t + 128)
-            mm([hb, c_at[h]], ps[:, 32 * t:32 * t + 32], w, S("hb"), True, False)
+    for h, bank in enumerate(("psu0", "psu1", "psd", "psf")):
+        ps = T[bank]
+        for t in range(4):
+            w = S("at", 512 * h + 128 * t, 512 * h + 128 * t + 128)
+            mm([hb, c_at[h // 2]], ps[:, 32 * t:32 * t + 32], w, S("hb"), True, False)
             r = mm([lb], ps[:, 32 * t:32 * t + 32], w, S("lb"), False, True)
-        pr = tt([r, c_b01], S("pr", 256 * h, 256 * h + 256), ps[:, 0:256], S("b01", 256 * h, 256 * h + 256), OP.mult)
-        for t in range(8):
-            c0, col = 256 * h + 32 * t, 8 * h + t
-            if t < 5:
+        pr = tt([r, c_b01], S("pr", 128 * h, 128 * h + 128), ps[:, 0:128], S("b01", 128 * h, 128 * h + 128), OP.mult)
+        for t in range(4):
+            c0, col = 128 * h + 32 * t, 4 * h + t
+            if t < 3:
                 wait("v", [pr])
                 sums.append(done("v", g.vector.tensor_reduce(S("mf", col, col + 1), S("pr", c0, c0 + 32), AxisListType.X, OP.add)))
             else:
                 sums.append(act([pr], S("junk", c0, c0 + 32), S("pr", c0, c0 + 32), AF.Copy, accum_out=S("mf", col, col + 1)))
     m = ts(sums, S("m"), S("mf"), BIAS, None, OP.add)
 
-    lo, hi, nl, pre = slots("2", S("m"), [m], TSH)
-    r = compact("2", lo, hi, nl, pre)
-    q = cp([r], T.q3[:], T.pse[:, 0:32])
+    r = compact("2", *slots("2", S("m"), [m], TSH))
+    q = cp([r], T.q3[:], T.pse[:, 0:64])
     got3 = spread(3, T.q3, q)
-    a = ts([], S("o256"), S("own2"), 256.0, None, OP.mult)
+    a = ts([], S("o256"), S("own2"), 256.0, -1.0, OP.mult, OP.add)
     a = tt([a], S("sl"), S("o256"), S("rk2"), OP.add)
     a = cp([a], T.slu[:], S("sl"))
     a = dma([a], T.ysl[:], T.slu[:], "dy1")
@@ -353,7 +369,9 @@ def rank_program(g, core, T, topo):
         yo = dma([a], T.yoff[16 * j:16 * j + 16, :], T.ysl[:], "dy2")
 
     for pg in range(8):
-        r = mm(got3 + [c_s8], T.psf[:, pg:256:8], S("s8", 128 * pg, 128 * pg + 128), T.l3[:, ck::4])
+        s8 = S("s8", 128 * pg, 128 * pg + 128)
+        mm(got3 + [c_s8], T.psf[:, pg:256:8], s8, T.l3[:, 2 * ck::8], True, False)
+        r = mm([], T.psf[:, pg:256:8], s8, T.l3[:, 2 * ck + 1::8], False, True)
     of = cp([r], S("off"), T.psf[:, 0:256])
 
     def gather(eng, c0, c1, out):
@@ -367,13 +385,15 @@ def rank_program(g, core, T, topo):
     for d in (opp[ci][0], same[ci][0], opp[ci][1], ci):
         if d != ci:
             c0 = 64 * d
-            tv = gather("v", c0, c0 + 32, T.gout[:, 16 * c0:16 * c0 + 512])
-            ta = gather("a", c0 + 32, c0 + 64, T.gout[:, 16 * c0 + 512:16 * c0 + 1024])
-            wait("p", [tv, ta])
+            half = [gather("v", c0, c0 + 32, T.gout[:, 16 * c0:16 * c0 + 512]),
+                    gather("a", c0 + 32, c0 + 64, T.gout[:, 16 * c0 + 512:16 * c0 + 1024])]
             via = relay[ci, ck, d]
             if via is not None:
-                fused([(T.gout[:, 1024 * d:1024 * d + 1024], T.rel[:], [via], 8, "c")], "s4")
+                for z, (a, b) in enumerate(pieces(ci, ck, d)):
+                    wait("p", half[a // 512:b // 512])
+                    fused([(T.gout[:, 1024 * d + a:1024 * d + b], T.rel[:, a:b], [via], 8, "c%d" % z)], "s4")
             else:
+                wait("p", half)
                 fused([(T.gout[:, 1024 * d + 256 * j:1024 * d + 256 * j + 256], T.recv[:, 256 * o:256 * o + 256],
                         [ranks[d][j]], 2, "col") for j in range(4)], "s4")
         else:
@@ -389,7 +409,12 @@ def rank_program(g, core, T, topo):
             wait("p", toks)
             fused([(T.gout[:, 1024 * d + 256 * j:1024 * d + 256 * j + 256], T.recv[:, 256 * o:256 * o + 256],
                     [ranks[d][j]], 4, "col") for j in range(4) if j != ck], "s4")
-    total["col"] = 3 * 4 + 12 * 2
+    total["col"] = 4 * 3
+    for i in range(n):
+        for k in range(4):
+            if i != ci:
+                whole = relay[i, k, ci] is None or len(pieces(i, k, ci)) == 1
+                total["col"] += 2 if whole else 4
 
     arrived = mine_tok + [("col", total["col"]), yo]
     for j in range(4):

@@ -1,10 +1,10 @@
 from concourse.bass import DstId, RemoteDMATransfer
-from concourse.mybir import AluOpType as OP, AxisListType, ActivationFunctionType as AF
+from concourse.mybir import AluOpType as OP, ActivationFunctionType as AF
 
 NC = 112
 MSH, TSH = 18, 14
 BIAS = float((1 << 17) + 256)
-BY_S = 12
+BY_V = (2, 4, 7, 9, 12, 14, 15)
 
 SCRATCH = {
     "x": ("sbuf", [128, 16], "int32"), "win": ("sbuf", [128, 8192], "int32"), "tabs": ("sbuf", [128, 16384], "bfloat16"),
@@ -13,21 +13,23 @@ SCRATCH = {
     "ysl": ("dram", [16, 128], "uint16"), "pst": ("psum", [128, 2048], "bfloat16"),
     "q1": ("sbuf", [128, 32], "int32"), "q2": ("sbuf", [128, 32], "int32"), "q3": ("sbuf", [128, 64], "bfloat16"),
     "gw1": ("sbuf", [128, 32], "int32"), "gw2": ("sbuf", [128, 32], "int32"), "gw3": ("sbuf", [128, 64], "bfloat16"),
+    "su4": ("sbuf", [128, 256], "float32"), "dmk": ("sbuf", [128, 512], "bfloat16"), "s8b": ("sbuf", [128, 1024], "bfloat16"),
     "l1": ("sbuf", [128, 128], "int32"), "l2": ("sbuf", [128, 128], "int32"), "l3": ("sbuf", [128, 256], "bfloat16"),
 }
 for _n in ("psb", "pse", "psu0", "psu1", "psd", "psf"):
     SCRATCH[_n] = ("psum", [128, 512], "float32")
 _INT = dict(ip=16, ip15=16, b32=32, ci=32, yq=32, yh=32, ya=32, yb=32, mh=32, ml=32, m=16)
-_FLT = dict(pcol=16, p16=16, key=256, su=256, lpat=512, dmask=512, cf=32, gat=1024, gt=1024,
-            ff=512, f1=512, pr=512, junk=512, mf=16, o256=16, sl=16)
-_BF = dict(iom1=128, io0=32, io32p=32, opat=256, d0=512, low=128, ident=128, at=2048, b01=512, hb=32, lb=32, key8=1024, s8=1024)
+_FLT = dict(pcol=16, p16=16, key=256, cf=32, gat=1024, gt=1024,
+            ff=512, f1=512, pr=768, junk=768, o256=16, sl=16)
+_BF = dict(iom1=128, io0=64, io32p=32, opat=256, d0=512, low=128, ident=128, at=2048, b01=768, hl=64, d32=128, d64=256, lpat=512,
+           key8=256)
 _U16 = dict(offt=16, coff=64, o2=32, off=256)
 for _f in "12":
     for _n in ("own", "hh", "ll"):
         _INT[_n + _f] = 16
     for _n in ("vh", "vl", "rk", "g16", "gm", "hi", "lo"):
         _FLT[_n + _f] = 16
-    for _n, _w in dict(oh=256, s1=256, ohb=256, cc=256, pm=128, ta=128, tb=64, tc=32, oa=2048, bb=1024, bo=512).items():
+    for _n, _w in dict(oh=256, s1=256, ohb=256, cc=256, pm=128, ta=64, tb=64, tc=32, oa=2048, bb=1024, bo=512).items():
         _BF[_n + _f] = _w
 PACK = {}
 for _buf, _ty, _d in (("pint", "int32", _INT), ("pflt", "float32", _FLT), ("pbf", "bfloat16", _BF), ("pu", "uint16", _U16)):
@@ -36,8 +38,8 @@ for _buf, _ty, _d in (("pint", "int32", _INT), ("pflt", "float32", _FLT), ("pbf"
         PACK[_n] = (_buf, _o, _w)
         _o += _w
     SCRATCH[_buf] = ("sbuf", [128, _o], _ty)
-SEMAPHORES = ["v", "a", "t", "p", "dx", "dm", "dt", "dy1", "dy2", "do", "i1", "i2",
-              "s1", "s2", "s3", "s4", "g1", "g2", "g3", "c0", "c1", "r1", "r2", "r3", "col", "sg"]
+SEMAPHORES = ["v", "a", "t", "p", "dx", "dm", "dn", "dt", "dy1", "dy2", "do", "i1", "i2",
+              "s1", "s2", "s3", "s4", "g1", "g2", "g3", "c0", "c1", "c2", "c3", "r1", "r2", "r3", "col", "sg", "k1", "k2", "sk"]
 
 
 def layout(T, topo):
@@ -72,7 +74,7 @@ def layout(T, topo):
                     gate[1, i, k, d] = rel[d][2 * w + k // 2]
                     gate[2, i, k, d] = gate[3, i, k, d] = hm[i][opp[i].index(d)]
                     relay[i, k, d] = rel[d][2 * w + cant.index(k)] if k in cant else None
-    return ranks, same, opp, gate, relay
+    return ranks, same, opp, gate, relay, helpers, rel
 
 
 def bits(m):
@@ -80,18 +82,19 @@ def bits(m):
 
 
 def rank_program(g, core, T, topo):
-    ranks, same, opp, gate, relay = layout(T, topo)
+    ranks, same, opp, gate, relay, helpers, rel = layout(T, topo)
     n = len(ranks)
     total = {}
     blk = {1: 8, 2: 8, 3: 16}
 
-    def fused(moves, local):
+    def fused(moves, local, like=None):
         used, out = [], {}
         order = sorted(range(len(moves)), key=lambda j: len(bits(topo.mask(core, moves[j][2][0]))))
         for j in order:
             src, dst, dsts, ne, sem = moves[j]
-            free = [b for b in bits(topo.mask(core, dsts[0])) if b not in used]
-            leaves = topo.chip(dsts[0]) != topo.chip(core)
+            way = dsts[0] if like is None else like
+            free = [b for b in bits(topo.mask(core, way)) if b not in used]
+            leaves = topo.chip(way) != topo.chip(core)
             take = free[:ne] if leaves else free[len(free) - ne:]
             used.extend(take)
             ids = []
@@ -107,10 +110,43 @@ def rank_program(g, core, T, topo):
         return 8 if d in same[i] else 4
 
     def pieces(i, k, d):
-        return [(0, 512), (512, 1024)] if d == opp[i][1] else [(0, 1024)]
+        last = d == opp[i][1 - k % 2]
+        if relay[i, k, d] is None:
+            return [(0, 1024)] if last else [(0, 512), (512, 1024)]
+        return [(256 * j, 256 * j + 256) for j in range(4)] if last else [(0, 512), (512, 1024)]
+
+    def S(name, a=0, b=None, st=1):
+        buf, o, w = PACK[name]
+        hi = o + (w if b is None else b)
+        return T[buf][:, o + a:hi] if st == 1 else T[buf][:, o + a:hi:st]
 
     rank = T.rank_of(core)
     if rank is None:
+        for i in range(n):
+            if core in helpers[i] + rel[i]:
+                near = core in helpers[i]
+                to = ranks[i][(helpers if near else rel)[i].index(core)]
+                if near:
+                    g.iota(S("ip"), [[0, 16]], 0, 1).then_inc(T.sem.p, 1)
+                    g.iota(S("lpat"), [[0, 32], [1, 16]], 0, 0, allow_small_or_imprecise_dtypes=True).then_inc(T.sem.p, 1)
+                    g.vector.wait_ge(T.sem.p, 2)
+                    g.vector.tensor_scalar(S("ip15"), S("ip"), 15, None, OP.bitwise_and).then_inc(T.sem.v, 1)
+                    g.vector.wait_ge(T.sem.v, 1)
+                    g.vector.tensor_copy(S("p16"), S("ip15")).then_inc(T.sem.v, 1)
+                    g.vector.wait_ge(T.sem.v, 2)
+                    g.vector.tensor_scalar(T.dmk[:], S("lpat"), S("p16", 0, 1), None, OP.is_equal).then_inc(T.sem.v, 1)
+                    g.wait_ge(T.sem.v, 3)
+                    move = (T.dmk[:], T.dmk[:], [to], 8, "k2")
+                else:
+                    g.iota(S("pcol"), [[0, 16]], 1, 1, allow_small_or_imprecise_dtypes=True).then_inc(T.sem.p, 1)
+                    for u in (0, 1):
+                        g.iota(S("key", 128 * u, 128 * u + 128), [[32, 4], [0, 2], [1, 16]], 16 * u + 1, 0,
+                               allow_small_or_imprecise_dtypes=True).then_inc(T.sem.p, 1)
+                    g.vector.wait_ge(T.sem.p, 3)
+                    g.vector.tensor_scalar(T.su4[:], S("key"), S("pcol", 0, 1), None, OP.is_equal).then_inc(T.sem.v, 1)
+                    g.wait_ge(T.sem.v, 1)
+                    move = (T.su4[:], T.su4[:], [to], 8, "k2")
+                fused([move], "sg", ranks[same[i][0]][0])
         for ph in (1, 2, 3):
             w = blk[ph]
             for i in range(n):
@@ -138,11 +174,6 @@ def rank_program(g, core, T, topo):
     ci, ck = rank // 4, rank % 4
     que = {"v": g.vector, "a": g.scalar, "t": g.tensor, "p": g, "s": g.sync}
     seen = {}
-
-    def S(name, a=0, b=None, st=1):
-        buf, o, w = PACK[name]
-        hi = o + (w if b is None else b)
-        return T[buf][:, o + a:hi] if st == 1 else T[buf][:, o + a:hi:st]
 
     def wait(q, deps):
         for s, c in deps:
@@ -196,37 +227,39 @@ def rank_program(g, core, T, topo):
 
     dx = dma([], T.x[:], T.idx[:], "dx")
 
-    def load_map(lo, hi):
-        for j in range(lo, hi):
-            h, a = j // 4, j % 4
-            p = 32 * a + 16 * h
-            r = dma([], T.win[p:p + 16, :], T.mp[:, 8192 * h:8192 * h + 8192], "dm")
+    def load_map(sem, quarters, lo):
+        for a in quarters:
+            for h in (0, 1):
+                p = 32 * a + 16 * h
+                r = dma([], T.win[p:p + 16, lo:8192], T.mp[:, 8192 * h + lo:8192 * h + 8192], sem)
         return r
 
     def load_tab(lo, hi):
         for j in range(lo, hi):
             r = dma([], T.tabs[:, 4096 * j:4096 * j + 4096], T.tab[:, 4096 * j:4096 * j + 4096], "dt")
         return r
-    load_map(0, 6)
+    dm = load_map("dm", (0, 1), 0)
 
     k_ip = iota(S("ip"), [[0, 16]], 0, 1)
-    k_op = iota(S("opat"), [[1, 16], [0, 16]], 0, 0)
+    k_k8 = iota(S("key8"), [[16, 2], [0, 8], [1, 16]], 32 * ck + 1, 0)
     k_io = iota(S("iom1"), [[1, 128]], 1, 0)
+    k_op = iota(S("opat"), [[1, 16], [0, 16]], 0, 0)
     k_ipp = iota(S("io32p"), [[4, 4], [16, 2], [1, 4]], 0, 0)
-    k_io0 = iota(S("io0"), [[1, 32]], 0, 0)
-    k_key = [iota(S("key", 128 * u, 128 * u + 128), [[32, 4], [0, 2], [1, 16]], 16 * u + 1, 0) for u in (0, 1)]
-    k_b32 = iota(S("b32"), [[32, 32]], 0, 0)
-    k_lp = iota(S("lpat"), [[0, 32], [1, 16]], 0, 0)
-    k_k8 = iota(S("key8"), [[16, 8], [0, 8], [1, 16]], 1, 0)
-    c = fill([], S("d0"), 1.0)
-    c_d0 = fill([c], S("d0", 0, 512, 16), 0.0)
     t1 = ts([k_ip], S("ip15"), S("ip"), 15, None, OP.bitwise_and)
     c_pc = ts([], S("pcol"), S("ip"), 1.0, None, OP.add)
     c_of = cp([t1], S("offt"), S("ip15"))
-    c_p16 = cp([], S("p16"), S("ip15"))
     pcol = S("pcol", 0, 1)
+    sib = [c for c in ranks[ci] if c != core]
+    own8 = T.s8b[:, 256 * ck:256 * ck + 256]
+    c_s8 = ts([k_k8, c_pc], own8, S("key8"), pcol, None, OP.is_equal)
+    c = fill([], S("d0"), 1.0)
+    c_d0 = fill([c], S("d0", 0, 512, 16), 0.0)
     c_low = ts([k_io, c_pc], S("low"), S("iom1"), pcol, None, OP.is_gt)
     c_id = ts([], S("ident"), S("iom1"), pcol, None, OP.is_equal)
+    wait("p", [c_s8])
+    fused([(own8, own8, [sib[j]], (8, 4, 4)[j], "k1") for j in range(3)], "sk")
+    total["k1"] = sum(8 if core == [c for c in ranks[ci] if c != s][0] else 4 for s in sib)
+    total["k2"] = 8 + 8
 
     def slots(f, x, dep, sh):
         a = ts(dep, S("own" + f), x, sh, None, OP.logical_shift_right)
@@ -239,14 +272,15 @@ def rank_program(g, core, T, topo):
         pb, z = sh // 2, (-256.0 if f == "1" else 0.0)
         ph = ts([], S("hh" + f), x, pb, (1 << pb) - 1, OP.logical_shift_right, OP.bitwise_and)
         pl = ts([], S("ll" + f), x, (1 << pb) - 1, None, OP.bitwise_and)
+        i = tt([d, e], ohb0, ohb0, T.psb[:, 0:16], OP.add)
         vh = ts([ph], S("vh" + f), S("hh" + f), z, float(1 << pb), OP.add, OP.mult)
         vl = ts([pl], S("vl" + f), S("ll" + f), z, None, OP.add)
-        i = tt([d, e], ohb0, ohb0, T.psb[:, 0:16], OP.add)
         j = scan([i], S("cc" + f), S("d0", 0, 256), S("ohb" + f))
         tt([j, ohp], S("pm" + f), T.psu0[:, 0:128], S("cc" + f, 0, 128), OP.mult)
         k = tt([], T.psu1[:, 0:128], T.psu0[:, 128:256], S("cc" + f, 128, 256), OP.mult)
-        k = tt([k], S("ta" + f), S("pm" + f), T.psu1[:, 0:128], OP.add)
-        k = tt([k], S("tb" + f), S("ta" + f, 0, 64), S("ta" + f, 64, 128), OP.add)
+        tt([k], S("ta" + f), S("pm" + f, 0, 64), T.psu1[:, 0:64], OP.add)
+        k = tt([], T.psu1[:, 128:192], S("pm" + f, 64, 128), T.psu1[:, 64:128], OP.add)
+        k = tt([k], S("tb" + f), S("ta" + f), T.psu1[:, 128:192], OP.add)
         k = tt([k], S("tc" + f), S("tb" + f, 0, 32), S("tb" + f, 32, 64), OP.add)
         k = tt([k], S("rk" + f), S("tc" + f, 0, 16), S("tc" + f, 16, 32), OP.add)
         gm = ts([k], S("gm" + f), S("rk" + f), 129.0, -128.0, OP.is_ge, OP.mult)
@@ -260,7 +294,7 @@ def rank_program(g, core, T, topo):
             oa, bo = S("oa" + f, 128 * t, 128 * t + 128), S("bo" + f, 32 * t, 32 * t + 32)
             bh, bl = S("bb" + f, 64 * t, 64 * t + 64, 2), S("bb" + f, 64 * t + 1, 64 * t + 64, 2)
             h, ch, cl = S("hi" + f, t, t + 1), S("vh" + f, t, t + 1), S("vl" + f, t, t + 1)
-            if t < BY_S:
+            if t not in BY_V:
                 b = ts([hi, k_ipp], bo, S("io32p"), h, None, OP.is_equal)
                 ta = ts([lo], oa, S("iom1"), S("lo" + f, t, t + 1), None, OP.is_equal)
                 th = act([b, vh], bh, bo, AF.Copy, scale=ch)
@@ -278,7 +312,6 @@ def rank_program(g, core, T, topo):
 
     def spread(ph, q, dep):
         land, w = T["l%d" % ph], blk[ph]
-        sib = [c for c in ranks[ci] if c != core]
         moves = []
         for d in opp[ci] + same[ci]:
             r = gate[ph, ci, ck, d]
@@ -299,35 +332,40 @@ def rank_program(g, core, T, topo):
     q = ts([r], T.q1[:], T.pse[:, 0:32], BIAS, None, OP.add)
     got1 = spread(1, T.q1, q)
     issued("i1")
-    dm = load_map(6, 8)
+    dn = load_map("dn", (2, 3), 4096)
     load_tab(0, 2)
+    k_io0 = iota(S("io0"), [[0, 2], [1, 32]], 0, 0)
+    k_b32 = iota(S("b32"), [[32, 32]], 0, 0)
+    c_win = cp([dm], T.win[64:128, 0:4096], T.win[0:64, 0:4096])
+    c = fill([], S("d32"), 1.0)
+    fill([c], S("d32", 0, 128, 32), 0.0)
+    c = fill([], S("d64"), 1.0)
+    c_d64 = fill([c], S("d64", 0, 256, 64), 0.0)
     tr = []
     for t in range(16):
         wait("t", [c_id])
         tr.append(done("t", g.tensor.transpose(T.pst[:, 128 * t:128 * t + 128], S("oa1", 128 * t, 128 * t + 128), S("ident"))))
     c_at = [act([tr[8 * h + 7]], S("at", 1024 * h, 1024 * h + 1024), T.pst[:, 1024 * h:1024 * h + 1024], AF.Copy) for h in (0, 1)]
-    c_su = [ts([k_key[u]], S("su", 128 * u, 128 * u + 128), S("key", 128 * u, 128 * u + 128), pcol, None, OP.is_equal)
-            for u in (0, 1)]
-    c_dm = ts([k_lp, c_p16], S("dmask"), S("lpat"), S("p16", 0, 1), None, OP.is_equal)
     for t in range(16):
-        c_b01 = ts([k_io0], S("b01", 32 * t, 32 * t + 32), S("io0"), S("hi1", t, t + 1), None, OP.is_equal)
-    c_s8 = ts([k_k8], S("s8"), S("key8"), pcol, None, OP.is_equal)
+        a, b = (64 * t, 64 * t + 64) if t < 8 else (256 + 32 * t, 288 + 32 * t)
+        c_b01 = ts([k_io0], S("b01", a, b), S("io0", 0, b - a), S("hi1", t, t + 1), None, OP.is_equal)
 
     mine = T.l1[:, ck::4]
+    consts = ("k2", total["k2"])
     a = ts(got1, S("ci"), mine, 4, 8191, OP.logical_shift_right, OP.bitwise_and)
     b = cp([a], S("cf"), S("ci"))
     for u in (0, 1):
-        d = mm([b, c_su[u]], T.psd[:, u:64:2], S("su", 128 * u, 128 * u + 128), S("cf"))
+        d = mm([b, consts], T.psd[:, u:64:2], T.su4[:, 128 * u:128 * u + 128], S("cf"))
     y1 = ts([], S("yq"), mine, 15, None, OP.bitwise_and)
     y2 = ts([], S("yh"), mine, 13, 16, OP.logical_shift_right, OP.bitwise_and)
     y3 = tt([y1, k_b32], S("ya"), S("yq"), S("b32"), OP.add)
     y4 = tt([y3, y2], S("yb"), S("ya"), S("yh"), OP.add)
     e = cp([d], S("coff"), T.psd[:, 0:64])
     y5 = cp([y4], S("o2"), S("yb"))
-    a = cp([e, dm], S("gat"), T.win[:, 0:8192].indirect(S("coff")))
+    a = cp([e, dm, dn, c_win], S("gat"), T.win[:, 0:8192].indirect(S("coff")))
     wait("v", [a])
     a = done("v", g.vector.transpose(S("gt"), S("gat")))
-    a = tt([a, y5, c_dm], S("ff"), S("gt").indirect(S("o2")), S("dmask"), OP.mult)
+    a = tt([a, y5, consts], S("ff"), S("gt").indirect(S("o2")), T.dmk[:], OP.mult)
     a = scan([a], S("f1"), S("d0"), S("ff"))
     a = cp([a], T.q2[:], S("f1", 15, 512, 16))
     got2 = spread(2, T.q2, a)
@@ -339,24 +377,25 @@ def rank_program(g, core, T, topo):
         src = T.l2[:, 2 * ck + k::8]
         hs.append(ts(got2, S("mh", 16 * k, 16 * k + 16), src, 9, None, OP.logical_shift_right))
         ls.append(ts([], S("ml", 16 * k, 16 * k + 16), src, 511, None, OP.bitwise_and))
-    hb = ts(hs, S("hb"), S("mh"), -256.0, 512.0, OP.add, OP.mult)
-    lb = ts(ls, S("lb"), S("ml"), -256.0, None, OP.add)
+    ts(hs, S("hl", 0, 32), S("mh"), -256.0, 512.0, OP.add, OP.mult)
+    hl = ts(ls, S("hl", 32, 64), S("ml"), -256.0, None, OP.add)
     sums = []
     for h, bank in enumerate(("psu0", "psu1", "psd", "psf")):
         ps = T[bank]
+        w = 64 if h < 2 else 32
+        c0 = 256 * h if h < 2 else 256 + 128 * h
+        c1 = c0 + 4 * w
         for t in range(4):
-            w = S("at", 512 * h + 128 * t, 512 * h + 128 * t + 128)
-            mm([hb, c_at[h // 2]], ps[:, 32 * t:32 * t + 32], w, S("hb"), True, False)
-            r = mm([lb], ps[:, 32 * t:32 * t + 32], w, S("lb"), False, True)
-        pr = tt([r, c_b01], S("pr", 128 * h, 128 * h + 128), ps[:, 0:128], S("b01", 128 * h, 128 * h + 128), OP.mult)
-        for t in range(4):
-            c0, col = 128 * h + 32 * t, 4 * h + t
-            if t < 3:
-                wait("v", [pr])
-                sums.append(done("v", g.vector.tensor_reduce(S("mf", col, col + 1), S("pr", c0, c0 + 32), AxisListType.X, OP.add)))
+            turned = S("at", 512 * h + 128 * t, 512 * h + 128 * t + 128)
+            if w == 64:
+                r = mm([hl, c_at[0]], ps[:, 64 * t:64 * t + 64], turned, S("hl"), True, True)
             else:
-                sums.append(act([pr], S("junk", c0, c0 + 32), S("pr", c0, c0 + 32), AF.Copy, accum_out=S("mf", col, col + 1)))
-    m = ts(sums, S("m"), S("mf"), BIAS, None, OP.add)
+                mm([hl, c_at[1]], ps[:, 32 * t:32 * t + 32], turned, S("hl", 0, 32), True, False)
+                r = mm([], ps[:, 32 * t:32 * t + 32], turned, S("hl", 32, 64), False, True)
+        pr = tt([r, c_b01], S("pr", c0, c1), ps[:, 0:4 * w], S("b01", c0, c1), OP.mult)
+        sums.append(scan([pr, c_d64], S("junk", c0, c1), S("d64" if w == 64 else "d32"), S("pr", c0, c1)))
+    ts(sums, S("m", 0, 8), S("junk", 63, 512, 64), BIAS, None, OP.add)
+    m = ts([], S("m", 8, 16), S("junk", 543, 768, 32), BIAS, None, OP.add)
 
     r = compact("2", *slots("2", S("m"), [m], TSH))
     q = cp([r], T.q3[:], T.pse[:, 0:64])
@@ -369,33 +408,34 @@ def rank_program(g, core, T, topo):
         yo = dma([a], T.yoff[16 * j:16 * j + 16, :], T.ysl[:], "dy2")
 
     for pg in range(8):
-        s8 = S("s8", 128 * pg, 128 * pg + 128)
-        mm(got3 + [c_s8], T.psf[:, pg:256:8], s8, T.l3[:, 2 * ck::8], True, False)
+        s8 = T.s8b[:, 128 * pg:128 * pg + 128]
+        mm(got3 + [c_s8, ("k1", total["k1"])], T.psf[:, pg:256:8], s8, T.l3[:, 2 * ck::8], True, False)
         r = mm([], T.psf[:, pg:256:8], s8, T.l3[:, 2 * ck + 1::8], False, True)
-    of = cp([r], S("off"), T.psf[:, 0:256])
+    turn = (opp[ci][ck % 2], same[ci][0], opp[ci][1 - ck % 2], ci)
+    of = {d: cp([r], S("off", 64 * d, 64 * d + 64), T.psf[:, 64 * d:64 * d + 64]) for d in turn}
 
     def gather(eng, c0, c1, out):
         src = T.tabs[:, 0:16384].indirect(S("off", c0, c1))
         if eng == "v":
-            return cp([of, dt], out, src)
-        return act([of, dt], out, src, AF.Copy)
+            return cp([of[c0 // 64], dt], out, src)
+        return act([of[c0 // 64], dt], out, src, AF.Copy)
 
     o = rank
     mine_tok = []
-    for d in (opp[ci][0], same[ci][0], opp[ci][1], ci):
+    for d in turn:
         if d != ci:
-            c0 = 64 * d
-            half = [gather("v", c0, c0 + 32, T.gout[:, 16 * c0:16 * c0 + 512]),
-                    gather("a", c0 + 32, c0 + 64, T.gout[:, 16 * c0 + 512:16 * c0 + 1024])]
             via = relay[ci, ck, d]
-            if via is not None:
-                for z, (a, b) in enumerate(pieces(ci, ck, d)):
-                    wait("p", half[a // 512:b // 512])
-                    fused([(T.gout[:, 1024 * d + a:1024 * d + b], T.rel[:, a:b], [via], 8, "c%d" % z)], "s4")
-            else:
+            for z, (a, b) in enumerate(pieces(ci, ck, d)):
+                c0, w = 64 * d + a // 16, (b - a) // 32
+                half = [gather("v", c0, c0 + w, T.gout[:, 16 * c0:16 * (c0 + w)]),
+                        gather("a", c0 + w, c0 + 2 * w, T.gout[:, 16 * (c0 + w):16 * (c0 + 2 * w)])]
                 wait("p", half)
-                fused([(T.gout[:, 1024 * d + 256 * j:1024 * d + 256 * j + 256], T.recv[:, 256 * o:256 * o + 256],
-                        [ranks[d][j]], 2, "col") for j in range(4)], "s4")
+                if via is not None:
+                    fused([(T.gout[:, 1024 * d + a:1024 * d + b], T.rel[:, a:b], [via], 8, "c%d" % z)], "s4")
+                else:
+                    js = range(a // 256, b // 256)
+                    fused([(T.gout[:, 1024 * d + 256 * j:1024 * d + 256 * j + 256], T.recv[:, 256 * o:256 * o + 256],
+                            [ranks[d][j]], 8 // len(js), "col") for j in js], "s4")
         else:
             toks = []
             for j in range(4):
@@ -413,8 +453,7 @@ def rank_program(g, core, T, topo):
     for i in range(n):
         for k in range(4):
             if i != ci:
-                whole = relay[i, k, ci] is None or len(pieces(i, k, ci)) == 1
-                total["col"] += 2 if whole else 4
+                total["col"] += [8 // ((q - p) // 256) for p, q in pieces(i, k, ci) if p <= 256 * ck < q][0]
 
     arrived = mine_tok + [("col", total["col"]), yo]
     for j in range(4):

from concourse.bass import DstId, RemoteDMATransfer
from concourse.mybir import AluOpType as OP, ActivationFunctionType as AF

NC = 112
MSH, TSH = 18, 14
BIAS = float((1 << 17) + 256)
BY_V = (2, 4, 7, 9, 12, 14, 15)

SCRATCH = {
    "x": ("sbuf", [128, 16], "int32"), "win": ("sbuf", [128, 8192], "int32"), "tabs": ("sbuf", [128, 16384], "bfloat16"),
    "recv": ("sbuf", [128, 4096], "bfloat16"), "gout": ("sbuf", [128, 4096], "bfloat16"), "ys": ("sbuf", [128, 2048], "bfloat16"),
    "rel": ("sbuf", [128, 1024], "bfloat16"), "slu": ("sbuf", [128, 16], "uint16"), "yoff": ("sbuf", [128, 128], "uint16"),
    "ysl": ("dram", [16, 128], "uint16"), "pst": ("psum", [128, 2048], "bfloat16"),
    "q1": ("sbuf", [128, 32], "int32"), "q2": ("sbuf", [128, 32], "int32"), "q3": ("sbuf", [128, 64], "bfloat16"),
    "gw1": ("sbuf", [128, 32], "int32"), "gw2": ("sbuf", [128, 32], "int32"), "gw3": ("sbuf", [128, 64], "bfloat16"),
    "su4": ("sbuf", [128, 256], "float32"), "dmk": ("sbuf", [128, 512], "bfloat16"), "s8b": ("sbuf", [128, 1024], "bfloat16"),
    "l1": ("sbuf", [128, 128], "int32"), "l2": ("sbuf", [128, 128], "int32"), "l3": ("sbuf", [128, 256], "bfloat16"),
}
for _n in ("psb", "pse", "psu0", "psu1", "psd", "psf"):
    SCRATCH[_n] = ("psum", [128, 512], "float32")
_INT = dict(ip=16, ip15=16, b32=32, ci=32, yq=32, yh=32, ya=32, yb=32, mh=32, ml=32, m=16)
_FLT = dict(pcol=16, p16=16, key=256, cf=32, gat=1024, gt=1024,
            ff=512, f1=512, pr=768, junk=768, o256=16, sl=16)
_BF = dict(iom1=128, io0=64, io32p=32, opat=256, d0=512, low=128, ident=128, at=2048, b01=768, hl=64, d32=128, d64=256, lpat=512,
           key8=256)
_U16 = dict(offt=16, coff=64, o2=32, off=256)
for _f in "12":
    for _n in ("own", "hh", "ll"):
        _INT[_n + _f] = 16
    for _n in ("vh", "vl", "rk", "g16", "gm", "hi", "lo"):
        _FLT[_n + _f] = 16
    for _n, _w in dict(oh=256, s1=256, ohb=256, cc=256, pm=128, ta=64, tb=64, tc=32, oa=2048, bb=1024, bo=512).items():
        _BF[_n + _f] = _w
PACK = {}
for _buf, _ty, _d in (("pint", "int32", _INT), ("pflt", "float32", _FLT), ("pbf", "bfloat16", _BF), ("pu", "uint16", _U16)):
    _o = 0
    for _n, _w in _d.items():
        PACK[_n] = (_buf, _o, _w)
        _o += _w
    SCRATCH[_buf] = ("sbuf", [128, _o], _ty)
SEMAPHORES = ["v", "a", "t", "p", "dx", "dm", "dn", "dt", "dy1", "dy2", "do", "i1", "i2",
              "s1", "s2", "s3", "s4", "g1", "g2", "g3", "c0", "c1", "c2", "c3", "r1", "r2", "r3", "col", "sg", "k1", "k2", "sk"]


def layout(T, topo):
    chips = []
    for c in T.cores:
        if topo.chip(c) not in chips:
            chips.append(topo.chip(c))
    nch = topo.chip(NC - 1) + 1
    ranks = [[c for c in T.cores if topo.chip(c) == x] for x in chips]
    on = {x: [c for c in range(NC) if topo.chip(c) == x] for x in range(nch)}
    mate = [[x for x in range(nch) if topo.mates(ch, x)][0] for ch in chips]
    n = len(chips)
    same = [[d for d in range(n) if d != i and topo.same_plane(chips[i], chips[d])] for i in range(n)]
    opp = [[d for d in range(n) if d != i and d not in same[i]] for i in range(n)]
    helpers = [[c for c in on[chips[i]] if topo.die(c) != topo.die(ranks[i][0])] for i in range(n)]
    hm = [[c for c in helpers[i] if topo.may_write(c, ranks[opp[i][0]][0])] for i in range(n)]
    hs = [[c for c in helpers[i] if c not in hm[i]] for i in range(n)]
    rel = [[c for c in on[mate[i]] if topo.may_write(c, ranks[i][0])] for i in range(n)]
    gate, relay = {}, {}
    for i in range(n):
        for d in range(n):
            if d == i:
                continue
            w = opp[d].index(i) if d in opp[i] else None
            cant = [k for k in range(4) if not topo.may_write(ranks[i][k], ranks[d][0])]
            for k in range(4):
                if w is None:
                    gate[1, i, k, d] = relay[i, k, d] = helpers[i][k]
                    gate[2, i, k, d] = hs[i][0]
                    gate[3, i, k, d] = hs[i][1]
                else:
                    gate[1, i, k, d] = rel[d][2 * w + k // 2]
                    gate[2, i, k, d] = gate[3, i, k, d] = hm[i][opp[i].index(d)]
                    relay[i, k, d] = rel[d][2 * w + cant.index(k)] if k in cant else None
    return ranks, same, opp, gate, relay, helpers, rel


def bits(m):
    return [b for b in range(m.bit_length()) if (m >> b) & 1]


def rank_program(g, core, T, topo):
    ranks, same, opp, gate, relay, helpers, rel = layout(T, topo)
    n = len(ranks)
    total = {}
    blk = {1: 8, 2: 8, 3: 16}

    def fused(moves, local, like=None):
        used, out = [], {}
        order = sorted(range(len(moves)), key=lambda j: len(bits(topo.mask(core, moves[j][2][0]))))
        for j in order:
            src, dst, dsts, ne, sem = moves[j]
            way = dsts[0] if like is None else like
            free = [b for b in bits(topo.mask(core, way)) if b not in used]
            leaves = topo.chip(way) != topo.chip(core)
            take = free[:ne] if leaves else free[len(free) - ne:]
            used.extend(take)
            ids = []
            for c in dsts:
                rid, pid, _e = topo.addr(c)
                ids.append(DstId(rid=rid, pnc=pid))
            out[j] = RemoteDMATransfer(dst_ids=ids, dma_engine_mask=sum(1 << b for b in take), remote_sem=T.sem[sem],
                                       srcs=[src], dsts=[dst] * len(dsts))
            total[local] = total.get(local, 0) + ne
        g.remote_dma_fused([out[j] for j in range(len(moves))], local_sem=T.sem[local])

    def hop1(i, d):
        return 8 if d in same[i] else 4

    def pieces(i, k, d):
        last = d == opp[i][1 - k % 2]
        if relay[i, k, d] is None:
            return [(0, 1024)] if last else [(0, 512), (512, 1024)]
        return [(256 * j, 256 * j + 256) for j in range(4)] if last else [(0, 512), (512, 1024)]

    def S(name, a=0, b=None, st=1):
        buf, o, w = PACK[name]
        hi = o + (w if b is None else b)
        return T[buf][:, o + a:hi] if st == 1 else T[buf][:, o + a:hi:st]

    rank = T.rank_of(core)
    if rank is None:
        for i in range(n):
            if core in helpers[i] + rel[i]:
                near = core in helpers[i]
                to = ranks[i][(helpers if near else rel)[i].index(core)]
                if near:
                    g.iota(S("ip"), [[0, 16]], 0, 1).then_inc(T.sem.p, 1)
                    g.iota(S("lpat"), [[0, 32], [1, 16]], 0, 0, allow_small_or_imprecise_dtypes=True).then_inc(T.sem.p, 1)
                    g.vector.wait_ge(T.sem.p, 2)
                    g.vector.tensor_scalar(S("ip15"), S("ip"), 15, None, OP.bitwise_and).then_inc(T.sem.v, 1)
                    g.vector.wait_ge(T.sem.v, 1)
                    g.vector.tensor_copy(S("p16"), S("ip15")).then_inc(T.sem.v, 1)
                    g.vector.wait_ge(T.sem.v, 2)
                    g.vector.tensor_scalar(T.dmk[:], S("lpat"), S("p16", 0, 1), None, OP.is_equal).then_inc(T.sem.v, 1)
                    g.wait_ge(T.sem.v, 3)
                    move = (T.dmk[:], T.dmk[:], [to], 8, "k2")
                else:
                    g.iota(S("pcol"), [[0, 16]], 1, 1, allow_small_or_imprecise_dtypes=True).then_inc(T.sem.p, 1)
                    for u in (0, 1):
                        g.iota(S("key", 128 * u, 128 * u + 128), [[32, 4], [0, 2], [1, 16]], 16 * u + 1, 0,
                               allow_small_or_imprecise_dtypes=True).then_inc(T.sem.p, 1)
                    g.vector.wait_ge(T.sem.p, 3)
                    g.vector.tensor_scalar(T.su4[:], S("key"), S("pcol", 0, 1), None, OP.is_equal).then_inc(T.sem.v, 1)
                    g.wait_ge(T.sem.v, 1)
                    move = (T.su4[:], T.su4[:], [to], 8, "k2")
                fused([move], "sg", ranks[same[i][0]][0])
        for ph in (1, 2, 3):
            w = blk[ph]
            for i in range(n):
                for d in range(n):
                    ks = [k for k in range(4) if d != i and gate[ph, i, k, d] == core]
                    if ks:
                        g.wait_ge(T.sem["g%d" % ph], hop1(i, d) * len(ks))
                        a = w * (4 * i + ks[0])
                        fused([(T["gw%d" % ph][:, 0:w * len(ks)], T["l%d" % ph][:, a:a + w * len(ks)], ranks[d], 8, "r%d" % ph)],
                              "sg")
        for i in range(n):
            for d in range(n):
                for k in range(4):
                    if d != i and relay[i, k, d] == core:
                        o = 4 * i + k
                        for z, (a, b) in enumerate(pieces(i, k, d)):
                            g.wait_ge(T.sem["c%d" % z], 8)
                            js = range(a // 256, b // 256)
                            fused([(T.rel[:, 256 * j:256 * j + 256], T.recv[:, 256 * o:256 * o + 256], [ranks[d][j]],
                                    8 // len(js), "col") for j in js], "sg")
        if "sg" in total:
            g.wait_ge(T.sem.sg, total["sg"])
        return

    ci, ck = rank // 4, rank % 4
    que = {"v": g.vector, "a": g.scalar, "t": g.tensor, "p": g, "s": g.sync}
    seen = {}

    def wait(q, deps):
        for s, c in deps:
            if seen.get((q, s), 0) < c:
                que[q].wait_ge(T.sem[s], c)
                seen[q, s] = c

    def done(q, ins):
        total[q] = total.get(q, 0) + 1
        ins.then_inc(T.sem[q], 1)
        return (q, total[q])

    def ts(deps, out, in0, s1, s2, op0, op1=None):
        wait("v", deps)
        if op1 is None:
            return done("v", g.vector.tensor_scalar(out, in0, s1, s2, op0))
        return done("v", g.vector.tensor_scalar(out, in0, s1, s2, op0, op1))

    def tt(deps, out, a, b, op):
        wait("v", deps)
        return done("v", g.vector.tensor_tensor(out, a, b, op))

    def cp(deps, out, a):
        wait("v", deps)
        return done("v", g.vector.tensor_copy(out, a))

    def fill(deps, out, c):
        wait("v", deps)
        return done("v", g.vector.memset(out, c))

    def scan(deps, out, a, b):
        wait("v", deps)
        return done("v", g.vector.tensor_tensor_scan(out, a, b, 0.0, OP.mult, OP.add))

    def mm(deps, out, l, r, start=True, stop=True):
        wait("t", deps)
        return done("t", g.tensor.matmul(out, l, r, start, stop))

    def act(deps, out, a, f, **kw):
        wait("a", deps)
        return done("a", g.scalar.activation(out, a, f, **kw))

    def iota(out, pattern, base, cm):
        return done("p", g.iota(out, pattern, base, cm, allow_small_or_imprecise_dtypes=True))

    def dma(deps, out, in_, sem):
        wait("s", deps)
        g.sync.dma_start(out, in_).then_inc(T.sem[sem], 16)
        total[sem] = total.get(sem, 0) + 16
        return (sem, total[sem])

    dx = dma([], T.x[:], T.idx[:], "dx")

    def load_map(sem, quarters, lo):
        for a in quarters:
            for h in (0, 1):
                p = 32 * a + 16 * h
                r = dma([], T.win[p:p + 16, lo:8192], T.mp[:, 8192 * h + lo:8192 * h + 8192], sem)
        return r

    def load_tab(lo, hi):
        for j in range(lo, hi):
            r = dma([], T.tabs[:, 4096 * j:4096 * j + 4096], T.tab[:, 4096 * j:4096 * j + 4096], "dt")
        return r
    dm = load_map("dm", (0, 1), 0)

    k_ip = iota(S("ip"), [[0, 16]], 0, 1)
    k_k8 = iota(S("key8"), [[16, 2], [0, 8], [1, 16]], 32 * ck + 1, 0)
    k_io = iota(S("iom1"), [[1, 128]], 1, 0)
    k_op = iota(S("opat"), [[1, 16], [0, 16]], 0, 0)
    k_ipp = iota(S("io32p"), [[4, 4], [16, 2], [1, 4]], 0, 0)
    t1 = ts([k_ip], S("ip15"), S("ip"), 15, None, OP.bitwise_and)
    c_pc = ts([], S("pcol"), S("ip"), 1.0, None, OP.add)
    c_of = cp([t1], S("offt"), S("ip15"))
    pcol = S("pcol", 0, 1)
    sib = [c for c in ranks[ci] if c != core]
    own8 = T.s8b[:, 256 * ck:256 * ck + 256]
    c_s8 = ts([k_k8, c_pc], own8, S("key8"), pcol, None, OP.is_equal)
    c = fill([], S("d0"), 1.0)
    c_d0 = fill([c], S("d0", 0, 512, 16), 0.0)
    c_low = ts([k_io, c_pc], S("low"), S("iom1"), pcol, None, OP.is_gt)
    c_id = ts([], S("ident"), S("iom1"), pcol, None, OP.is_equal)
    wait("p", [c_s8])
    fused([(own8, own8, [sib[j]], (8, 4, 4)[j], "k1") for j in range(3)], "sk")
    total["k1"] = sum(8 if core == [c for c in ranks[ci] if c != s][0] else 4 for s in sib)
    total["k2"] = 8 + 8

    def slots(f, x, dep, sh):
        a = ts(dep, S("own" + f), x, sh, None, OP.logical_shift_right)
        b = tt([a, c_of, k_op], S("oh" + f), S("own" + f).indirect(S("offt")), S("opat"), OP.is_equal)
        ohp = act([b], T.psu0[:, 0:256], S("oh" + f), AF.Copy)
        c = scan([b, c_d0], S("s1" + f), S("d0", 0, 256), S("oh" + f))
        d = mm([c, c_low], T.psb[:, 0:16], S("low"), S("s1" + f, 15, 256, 16))
        ohb0 = S("ohb" + f, 0, 256, 16)
        e = cp([], S("ohb" + f), S("oh" + f))
        pb, z = sh // 2, (-256.0 if f == "1" else 0.0)
        ph = ts([], S("hh" + f), x, pb, (1 << pb) - 1, OP.logical_shift_right, OP.bitwise_and)
        pl = ts([], S("ll" + f), x, (1 << pb) - 1, None, OP.bitwise_and)
        i = tt([d, e], ohb0, ohb0, T.psb[:, 0:16], OP.add)
        vh = ts([ph], S("vh" + f), S("hh" + f), z, float(1 << pb), OP.add, OP.mult)
        vl = ts([pl], S("vl" + f), S("ll" + f), z, None, OP.add)
        j = scan([i], S("cc" + f), S("d0", 0, 256), S("ohb" + f))
        tt([j, ohp], S("pm" + f), T.psu0[:, 0:128], S("cc" + f, 0, 128), OP.mult)
        k = tt([], T.psu1[:, 0:128], T.psu0[:, 128:256], S("cc" + f, 128, 256), OP.mult)
        tt([k], S("ta" + f), S("pm" + f, 0, 64), T.psu1[:, 0:64], OP.add)
        k = tt([], T.psu1[:, 128:192], S("pm" + f, 64, 128), T.psu1[:, 64:128], OP.add)
        k = tt([k], S("tb" + f), S("ta" + f), T.psu1[:, 128:192], OP.add)
        k = tt([k], S("tc" + f), S("tb" + f, 0, 32), S("tb" + f, 32, 64), OP.add)
        k = tt([k], S("rk" + f), S("tc" + f, 0, 16), S("tc" + f, 16, 32), OP.add)
        gm = ts([k], S("gm" + f), S("rk" + f), 129.0, -128.0, OP.is_ge, OP.mult)
        g16 = ts([], S("g16" + f), S("rk" + f), 129.0, 16.0, OP.is_ge, OP.mult)
        lo = tt([gm], S("lo" + f), S("gm" + f), S("rk" + f), OP.add)
        hi = tt([g16], S("hi" + f), S("g16" + f), S("own" + f), OP.add)
        return lo, hi, vh, vl

    def compact(f, lo, hi, vh, vl):
        for t in range(16):
            oa, bo = S("oa" + f, 128 * t, 128 * t + 128), S("bo" + f, 32 * t, 32 * t + 32)
            bh, bl = S("bb" + f, 64 * t, 64 * t + 64, 2), S("bb" + f, 64 * t + 1, 64 * t + 64, 2)
            h, ch, cl = S("hi" + f, t, t + 1), S("vh" + f, t, t + 1), S("vl" + f, t, t + 1)
            if t not in BY_V:
                b = ts([hi, k_ipp], bo, S("io32p"), h, None, OP.is_equal)
                ta = ts([lo], oa, S("iom1"), S("lo" + f, t, t + 1), None, OP.is_equal)
                th = act([b, vh], bh, bo, AF.Copy, scale=ch)
                tl = act([vl], bl, bo, AF.Copy, scale=cl)
            else:
                th = ts([hi, vh], bh, S("io32p"), h, ch, OP.is_equal, OP.mult)
                tl = ts([vl], bl, S("io32p"), h, cl, OP.is_equal, OP.mult)
                ta = ts([lo], oa, S("iom1"), S("lo" + f, t, t + 1), None, OP.is_equal)
            if f == "1":
                mm([ta, th], T.pse[:, 0:32], oa, bh, t == 0, False)
                r = mm([tl], T.pse[:, 0:32], oa, bl, False, t == 15)
            else:
                r = mm([ta, th, tl], T.pse[:, 0:64], oa, S("bb" + f, 64 * t, 64 * t + 64), t == 0, t == 15)
        return r

    def spread(ph, q, dep):
        land, w = T["l%d" % ph], blk[ph]
        moves = []
        for d in opp[ci] + same[ci]:
            r = gate[ph, ci, ck, d]
            a = w * (ck - min(k for k in range(4) if gate[ph, ci, k, d] == r))
            moves.append((q[:, w * d:w * d + w], T["gw%d" % ph][:, a:a + w], [r], hop1(ci, d), "g%d" % ph))
        wait("p", [dep])
        fused(moves, "s%d" % ph)
        fused([(q[:, w * ci:w * ci + w], land[:, w * rank:w * rank + w], sib, 8, "r%d" % ph)], "s%d" % ph)
        total["r%d" % ph] = 8 * len(sib) + 8 * sum(len(set(gate[ph, i, k, ci] for k in range(4))) for i in range(n) if i != ci)
        return [cp([dep], land[:, w * rank:w * rank + w], q[:, w * ci:w * ci + w]), ("r%d" % ph, total["r%d" % ph])]

    def issued(name):
        g.sem_inc(T.sem[name], 1)
        total[name] = 1
        wait("s", [(name, 1)])

    r = compact("1", *slots("1", T.x[:], [dx], MSH))
    q = ts([r], T.q1[:], T.pse[:, 0:32], BIAS, None, OP.add)
    got1 = spread(1, T.q1, q)
    issued("i1")
    dn = load_map("dn", (2, 3), 4096)
    load_tab(0, 2)
    k_io0 = iota(S("io0"), [[0, 2], [1, 32]], 0, 0)
    k_b32 = iota(S("b32"), [[32, 32]], 0, 0)
    c_win = cp([dm], T.win[64:128, 0:4096], T.win[0:64, 0:4096])
    c = fill([], S("d32"), 1.0)
    fill([c], S("d32", 0, 128, 32), 0.0)
    c = fill([], S("d64"), 1.0)
    c_d64 = fill([c], S("d64", 0, 256, 64), 0.0)
    tr = []
    for t in range(16):
        wait("t", [c_id])
        tr.append(done("t", g.tensor.transpose(T.pst[:, 128 * t:128 * t + 128], S("oa1", 128 * t, 128 * t + 128), S("ident"))))
    c_at = [act([tr[8 * h + 7]], S("at", 1024 * h, 1024 * h + 1024), T.pst[:, 1024 * h:1024 * h + 1024], AF.Copy) for h in (0, 1)]
    for t in range(16):
        a, b = (64 * t, 64 * t + 64) if t < 8 else (256 + 32 * t, 288 + 32 * t)
        c_b01 = ts([k_io0], S("b01", a, b), S("io0", 0, b - a), S("hi1", t, t + 1), None, OP.is_equal)

    mine = T.l1[:, ck::4]
    consts = ("k2", total["k2"])
    a = ts(got1, S("ci"), mine, 4, 8191, OP.logical_shift_right, OP.bitwise_and)
    b = cp([a], S("cf"), S("ci"))
    for u in (0, 1):
        d = mm([b, consts], T.psd[:, u:64:2], T.su4[:, 128 * u:128 * u + 128], S("cf"))
    y1 = ts([], S("yq"), mine, 15, None, OP.bitwise_and)
    y2 = ts([], S("yh"), mine, 13, 16, OP.logical_shift_right, OP.bitwise_and)
    y3 = tt([y1, k_b32], S("ya"), S("yq"), S("b32"), OP.add)
    y4 = tt([y3, y2], S("yb"), S("ya"), S("yh"), OP.add)
    e = cp([d], S("coff"), T.psd[:, 0:64])
    y5 = cp([y4], S("o2"), S("yb"))
    a = cp([e, dm, dn, c_win], S("gat"), T.win[:, 0:8192].indirect(S("coff")))
    wait("v", [a])
    a = done("v", g.vector.transpose(S("gt"), S("gat")))
    a = tt([a, y5, consts], S("ff"), S("gt").indirect(S("o2")), T.dmk[:], OP.mult)
    a = scan([a], S("f1"), S("d0"), S("ff"))
    a = cp([a], T.q2[:], S("f1", 15, 512, 16))
    got2 = spread(2, T.q2, a)
    issued("i2")
    dt = load_tab(2, 4)

    hs, ls = [], []
    for k in (0, 1):
        src = T.l2[:, 2 * ck + k::8]
        hs.append(ts(got2, S("mh", 16 * k, 16 * k + 16), src, 9, None, OP.logical_shift_right))
        ls.append(ts([], S("ml", 16 * k, 16 * k + 16), src, 511, None, OP.bitwise_and))
    ts(hs, S("hl", 0, 32), S("mh"), -256.0, 512.0, OP.add, OP.mult)
    hl = ts(ls, S("hl", 32, 64), S("ml"), -256.0, None, OP.add)
    sums = []
    for h, bank in enumerate(("psu0", "psu1", "psd", "psf")):
        ps = T[bank]
        w = 64 if h < 2 else 32
        c0 = 256 * h if h < 2 else 256 + 128 * h
        c1 = c0 + 4 * w
        for t in range(4):
            turned = S("at", 512 * h + 128 * t, 512 * h + 128 * t + 128)
            if w == 64:
                r = mm([hl, c_at[0]], ps[:, 64 * t:64 * t + 64], turned, S("hl"), True, True)
            else:
                mm([hl, c_at[1]], ps[:, 32 * t:32 * t + 32], turned, S("hl", 0, 32), True, False)
                r = mm([], ps[:, 32 * t:32 * t + 32], turned, S("hl", 32, 64), False, True)
        pr = tt([r, c_b01], S("pr", c0, c1), ps[:, 0:4 * w], S("b01", c0, c1), OP.mult)
        sums.append(scan([pr, c_d64], S("junk", c0, c1), S("d64" if w == 64 else "d32"), S("pr", c0, c1)))
    ts(sums, S("m", 0, 8), S("junk", 63, 512, 64), BIAS, None, OP.add)
    m = ts([], S("m", 8, 16), S("junk", 543, 768, 32), BIAS, None, OP.add)

    r = compact("2", *slots("2", S("m"), [m], TSH))
    q = cp([r], T.q3[:], T.pse[:, 0:64])
    got3 = spread(3, T.q3, q)
    a = ts([], S("o256"), S("own2"), 256.0, -1.0, OP.mult, OP.add)
    a = tt([a], S("sl"), S("o256"), S("rk2"), OP.add)
    a = cp([a], T.slu[:], S("sl"))
    a = dma([a], T.ysl[:], T.slu[:], "dy1")
    for j in range(8):
        yo = dma([a], T.yoff[16 * j:16 * j + 16, :], T.ysl[:], "dy2")

    for pg in range(8):
        s8 = T.s8b[:, 128 * pg:128 * pg + 128]
        mm(got3 + [c_s8, ("k1", total["k1"])], T.psf[:, pg:256:8], s8, T.l3[:, 2 * ck::8], True, False)
        r = mm([], T.psf[:, pg:256:8], s8, T.l3[:, 2 * ck + 1::8], False, True)
    turn = (opp[ci][ck % 2], same[ci][0], opp[ci][1 - ck % 2], ci)
    of = {d: cp([r], S("off", 64 * d, 64 * d + 64), T.psf[:, 64 * d:64 * d + 64]) for d in turn}

    def gather(eng, c0, c1, out):
        src = T.tabs[:, 0:16384].indirect(S("off", c0, c1))
        if eng == "v":
            return cp([of[c0 // 64], dt], out, src)
        return act([of[c0 // 64], dt], out, src, AF.Copy)

    o = rank
    mine_tok = []
    for d in turn:
        if d != ci:
            via = relay[ci, ck, d]
            for z, (a, b) in enumerate(pieces(ci, ck, d)):
                c0, w = 64 * d + a // 16, (b - a) // 32
                half = [gather("v", c0, c0 + w, T.gout[:, 16 * c0:16 * (c0 + w)]),
                        gather("a", c0 + w, c0 + 2 * w, T.gout[:, 16 * (c0 + w):16 * (c0 + 2 * w)])]
                wait("p", half)
                if via is not None:
                    fused([(T.gout[:, 1024 * d + a:1024 * d + b], T.rel[:, a:b], [via], 8, "c%d" % z)], "s4")
                else:
                    js = range(a // 256, b // 256)
                    fused([(T.gout[:, 1024 * d + 256 * j:1024 * d + 256 * j + 256], T.recv[:, 256 * o:256 * o + 256],
                            [ranks[d][j]], 8 // len(js), "col") for j in js], "s4")
        else:
            toks = []
            for j in range(4):
                c0 = 64 * d + 16 * j
                dst = T.recv[:, 256 * o:256 * o + 256] if j == ck else T.gout[:, 16 * c0:16 * c0 + 256]
                tk = gather("v" if j % 2 == 0 else "a", c0, c0 + 16, dst)
                if j == ck:
                    mine_tok.append(tk)
                else:
                    toks.append(tk)
            wait("p", toks)
            fused([(T.gout[:, 1024 * d + 256 * j:1024 * d + 256 * j + 256], T.recv[:, 256 * o:256 * o + 256],
                    [ranks[d][j]], 4, "col") for j in range(4) if j != ck], "s4")
    total["col"] = 4 * 3
    for i in range(n):
        for k in range(4):
            if i != ci:
                total["col"] += [8 // ((q - p) // 256) for p, q in pieces(i, k, ci) if p <= 256 * ck < q][0]

    arrived = mine_tok + [("col", total["col"]), yo]
    for j in range(4):
        src = T.recv[:, 0:4096].indirect(T.yoff[:, 32 * j:32 * j + 32])
        out = T.ys[:, 512 * j:512 * j + 512]
        tk = cp(arrived, out, src) if j % 2 == 0 else act(arrived, out, src, AF.Copy)
        dma([tk], T.y[:, 512 * j:512 * j + 512], out, "do")
    wait("p", [(s, total[s]) for s in total])
